import numpy as np
import ml_dtypes


def mxq(x, axis, fmt="e4m3"):
    dtype, down = {"e4m3": (ml_dtypes.float8_e4m3fn, 7), "e5m2": (ml_dtypes.float8_e5m2, 14)}[fmt]
    v = np.moveaxis(np.asarray(x, np.float32).astype(ml_dtypes.bfloat16).astype(np.float64), axis, -1)
    blocks = v.reshape(v.shape[:-1] + (-1, 32))
    amax = np.abs(blocks).max(-1, keepdims=True)
    byte = np.maximum(np.where(amax > 0, np.frexp(amax)[1] - 1 + 127, 0) - down, 1)
    scale = np.exp2(byte - 127.0)
    codes = (blocks / scale).astype(np.float32).astype(dtype).astype(np.float64)
    return np.moveaxis((codes * scale).reshape(v.shape), -1, axis)


WIDE = False


def mx_kscale(k):
    if not WIDE:
        return np.ones(k)
    levels = np.array([10, -10, 5, -5, 0])
    if k % 512:
        return np.exp2(np.random.permutation(np.resize(levels, k // 32))).repeat(32)
    a = np.empty((k // 512, 16))
    for p in range(k // 512):
        a[p, :8] = np.random.permutation(np.resize(levels, 8))
        for g in range(8):
            far = levels[np.abs(levels - a[p, g]) >= 10]
            a[p, g + 8] = far[np.random.randint(len(far))]
    return np.exp2(a.ravel()).repeat(32)


BF16 = ml_dtypes.bfloat16


def bf(x):
    return np.asarray(x, np.float32).astype(BF16)


def f64(x):
    return np.asarray(x).astype(np.float64)


E2M1 = np.array([0.0, 0.5, 1.0, 1.5, 2.0, 3.0, 4.0, 6.0, -0.0, -0.5, -1.0, -1.5, -2.0, -3.0, -4.0, -6.0])


def pack_weight(w, fmt):
    k, n = w.shape
    w = f64(bf(w)).reshape(k // 32, 32, n)
    amax = np.abs(w).max(1)
    if fmt == "e4m3":
        byte = np.frexp(amax)[1] - 1 + 127 - 7
    else:
        mant, ex = np.frexp(amax / 6.0)
        byte = np.where(mant > 0.5, ex, ex - 1) + 127
    byte = np.clip(np.where(amax > 0, byte, 1), 1, 254)
    scaled = (w * np.exp2(127.0 - byte)[:, None, :]).reshape(k, n).astype(np.float32)
    by_word = np.ascontiguousarray(scaled.reshape(k // 512, 128, 4, n).transpose(0, 1, 3, 2))
    if fmt == "e4m3":
        words = by_word.astype(ml_dtypes.float8_e4m3fn).view(np.uint8)
    else:
        c = by_word.astype(ml_dtypes.float4_e2m1fn).view(np.uint8) & 0xF
        words = c[..., 0::2] | (c[..., 1::2] << 4)
    return np.ascontiguousarray(words), np.ascontiguousarray(byte.astype(np.uint8).reshape(k // 512, 16, n))


def unpack_weight(words, scales, fmt):
    g, p, n, _ = words.shape
    if fmt == "e4m3":
        vals = np.ascontiguousarray(words).view(ml_dtypes.float8_e4m3fn).astype(np.float64)
    else:
        nib = np.empty((g, p, n, 4), np.uint8)
        nib[..., 0::2] = words & 0xF
        nib[..., 1::2] = words >> 4
        vals = E2M1[nib]
    vals = vals * np.repeat(np.exp2(scales.astype(np.float64) - 127.0), 8, axis=1)[..., None]
    return vals.transpose(0, 1, 3, 2).reshape(g * 512, n)
def pack4(w):
    words, scales = pack_weight(w, "e2m1")
    return words.reshape(words.shape[0], 128, -1), scales


def unpack4(words, scales):
    return unpack_weight(words.reshape(words.shape[0], 128, -1, 2), scales, "e2m1")


P, E, F, G, A = 2048, 1024, 1024, 8, 16
K = G * A
C = 2 * K
N = K - 1


def erf(a):
    c = np.clip(a, -6.0, 6.0)
    q = 2.0 * c * c
    term = c.copy()
    total = c.copy()
    for n in range(1, 150):
        term *= q
        term /= 2.0 * n + 1.0
        total += term
    return np.where(np.abs(a) > 6.0, np.sign(a), 2.0 / np.sqrt(np.pi) * np.exp(-c * c) * total)


def gelu_erf(v):
    return 0.5 * v * (1.0 + erf(v / np.sqrt(2.0)))


def softplus(v):
    return np.maximum(v, 0.0) + np.log(1.0 + np.exp(-np.abs(v)))


def log_binomial_stirling():
    eps = 1e-6
    n = float(N)
    k = np.arange(K, dtype=np.float64)
    lower = k + eps
    upper = n - k + eps
    return n * np.log(n) - lower * np.log(lower) - upper * np.log(upper)


def draw0():
    s, t = mx_kscale(E), mx_kscale(F)
    x = bf(np.random.standard_normal((P, E)) * s)
    w1_words, w1_scales = pack4(np.random.standard_normal((E, F)) / np.sqrt(E) / s[:, None])
    b1 = bf(np.random.standard_normal(F) * 0.3)
    g = bf(np.random.standard_normal(F) * t)
    w_head_words, w_head_scales = pack4(np.random.standard_normal((F, C)) * 2.0 / np.sqrt(F) / t[:, None])
    w_q = bf(np.random.standard_normal(F) / np.sqrt(F) / t)
    return {
        "x": x,
        "w1_words": w1_words,
        "w1_scales": w1_scales,
        "b1": b1,
        "g": g,
        "w_head_words": w_head_words,
        "w_head_scales": w_head_scales,
        "w_q": w_q,
    }


def core(x, w1_words, w1_scales, b1, g, w_head_words, w_head_scales, w_q):
    rows = x.shape[0]

    h = gelu_erf((mxq(f64(x), 1, "e4m3") @ unpack4(w1_words, w1_scales)) + f64(b1)) * f64(g)

    y = softplus(mxq(h, 1, "e4m3") @ unpack4(w_head_words, w_head_scales))
    c = y[:, :K].reshape(rows, G, A)
    a = y[:, K:C].reshape(rows, G, A)

    dx = a[:, :, None, :] - c[:, :, :, None]
    pull = np.mean(dx / (1.0 + 2.0 * dx ** 2), axis=-1)
    c2 = (c + 2.0 * pull).reshape(rows, K)

    u = np.sum(h * f64(w_q)[None, :], axis=-1)

    lc = log_binomial_stirling()

    k = np.arange(K, dtype=np.float64)
    logits = (lc[None, :] + k[None, :] * u[:, None]) / 20.0
    e = np.exp(logits - logits.max(axis=-1, keepdims=True))
    p = e / e.sum(axis=-1, keepdims=True)

    return K * p * c2


def e4m3fn_bytes(y):
    return np.clip(np.asarray(y, np.float64), -448.0, 448.0).astype(np.float32).astype(ml_dtypes.float8_e4m3fn).view(np.uint8)


def e4m3fn_values(b):
    return np.asarray(b, np.uint8).view(ml_dtypes.float8_e4m3fn).astype(np.float64)


def setup_inputs():
    d = draw0()
    x0 = np.asarray(d['x']).astype(np.float64)
    s = (np.max(np.abs(x0), axis=(0,), keepdims=True) / 448.0).astype(np.float32)
    out = {}
    for k, v in d.items():
        if k == 'x':
            out['x_bytes'] = e4m3fn_bytes(x0 / s.astype(np.float64))
            out['x_scale'] = s
        else:
            out[k] = v
    return out


def reference(x_bytes, x_scale, w1_words, w1_scales, b1, g, w_head_words, w_head_scales, w_q):
    return core(e4m3fn_values(x_bytes) * x_scale.astype(np.float64), w1_words, w1_scales, b1, g, w_head_words, w_head_scales, w_q)

@@ -1,0 +1,546 @@
+import math
+from contextlib import ExitStack
+
+import concourse.mybir as mybir
+from concourse.masks import make_identity
+
+F32 = mybir.dt.float32
+BF16 = mybir.dt.bfloat16
+I32 = mybir.dt.int32
+U32 = mybir.dt.uint32
+U8 = mybir.dt.uint8
+FP8 = mybir.dt.float8_e4m3fn
+FP8X4 = mybir.dt.float8_e4m3fn_x4
+FP4X4 = mybir.dt.float4_e2m1fn_x4
+ALU = mybir.AluOpType
+ACT = mybir.ActivationFunctionType
+AX = mybir.AxisListType
+
+P = 128
+T, E, F, K = 2048, 1024, 1024, 128
+CH = 512
+NCH = T // CH
+GAIN_S = {(c, 1) for c in range(NCH)}
+TPC = CH // P
+
+FLOPS = 2 * T * E * F + 2 * T * F * 2 * K
+
+
+def tile_attractordepthbinhead_w4_kernel(
+    tc, x_bytes, x_scale, w1_words, w1_scales, b1, g, w_head_words, w_head_scales, w_q, out
+):
+    nc = tc.nc
+    with ExitStack() as ctx:
+        const = ctx.enter_context(tc.tile_pool(name="const", bufs=1))
+        work = ctx.enter_context(tc.tile_pool(name="work", bufs=2))
+        psum = ctx.enter_context(tc.psum_pool(name="psum", bufs=1))
+        ctx.enter_context(tc.manual_schedule())
+
+        w1_raw = const.tile([P, 2, 2048], U8, name="w1_raw", align_bytes=64)
+        w1_perm = const.tile([P, 2, 2048], U8, name="w1_perm", align_bytes=64)
+        s1_raw = const.tile([P, 2, 1024], U8, name="s1_raw", align_bytes=64)
+        s1_perm = const.tile([P, 2, 1024], U8, name="s1_perm", align_bytes=64)
+        wh = const.tile([P, 2, 2, 256], U8, name="wh", align_bytes=64)
+        sh_raw = const.tile([P, 2, 256], U8, name="sh_raw", align_bytes=64)
+        sh = const.tile([P, 2, 256], U8, name="sh", align_bytes=64)
+        scale = const.tile([P, E], F32, name="scale")
+        xb = const.tile([P, T // P, E], U8, name="xb")
+        b1_t = const.tile([P, 8], BF16, name="b1_t")
+        g_t = const.tile([P, 8], BF16, name="g_t")
+        wq_t = const.tile([P, 8], BF16, name="wq_t")
+
+        nc.vector.memset(s1_raw[:].rearrange("p g n -> p (g n)").bitcast(I32), 0)
+        nc.vector.memset(sh_raw[:].rearrange("p g n -> p (g n)").bitcast(I32), 0)
+
+        nc.scalar.dma_start(out=scale[:], in_=x_scale.rearrange("o k -> (o k)").partition_broadcast(P))
+
+        def load_w1(half):
+            cols = slice(1024 * half, 1024 * half + 1024)
+            nc.sync.dma_start(out=w1_raw[:, :, cols], in_=w1_words[:, :, cols].rearrange("g p b -> p g b"))
+
+        x_rows = x_bytes.rearrange("(i p) k -> p i k", p=P)
+        for i in range(TPC):
+            nc.sync.dma_start(out=xb[:, i, :], in_=x_rows[:, i, :])
+        load_w1(0)
+        for q in range(4):
+            nc.sync.dma_start(
+                out=s1_raw[32 * q : 32 * q + 4, :, :].rearrange("r g n -> r (g n)").bitcast(I32).rearrange("r (g n) -> r g n", g=2),
+                in_=w1_scales.bitcast(I32)[:, 4 * q : 4 * q + 4, :].rearrange("g r n -> r g n"),
+            )
+        load_w1(1)
+        nc.sync.dma_start(out=b1_t[:].rearrange("p (g t) -> p g t", g=2), in_=b1.rearrange("(g p t) -> p g t", g=2, t=4))
+        nc.sync.dma_start(out=g_t[:].rearrange("p (g t) -> p g t", g=2), in_=g.rearrange("(g p t) -> p g t", g=2, t=4))
+        nc.sync.dma_start(out=wq_t[:].rearrange("p (g t) -> p g t", g=2), in_=w_q.rearrange("(g p t) -> p g t", g=2, t=4))
+        nc.sync.dma_start(out=xb[:, TPC : 2 * TPC, :], in_=x_rows[:, TPC : 2 * TPC, :])
+        for gg in range(2):
+            for h in range(2):
+                nc.sync.dma_start(
+                    out=wh[:, gg, h, :].rearrange("p (c b) -> p c b", c=2),
+                    in_=w_head_words[gg].rearrange("p (c h b) -> p h c b", c=2, h=2)[:, h],
+                )
+        for q in range(4):
+            nc.sync.dma_start(
+                out=sh_raw[32 * q : 32 * q + 4, :, :].rearrange("r g n -> r (g n)").bitcast(I32).rearrange("r (g n) -> r g n", g=2),
+                in_=w_head_scales.bitcast(I32)[:, 4 * q : 4 * q + 4, :].rearrange("g r n -> r g n"),
+            )
+        for c in range(2, NCH):
+            nc.sync.dma_start(out=xb[:, c * TPC : (c + 1) * TPC, :], in_=x_rows[:, c * TPC : (c + 1) * TPC, :])
+
+        ident = const.tile([P, P], F32, name="ident")
+        make_identity(nc, ident[:])
+        kv = const.tile([P, K], F32, name="kv")
+        nc.gpsimd.iota(kv[:], pattern=[[1, K]], base=0, channel_multiplier=0, allow_small_or_imprecise_dtypes=True)
+        dmat = const.tile([P, 8, 64], F32, name="dmat")
+        nc.gpsimd.tensor_scalar(
+            out=dmat[0:64],
+            in0=ident[0:64, 0:64].unsqueeze(1).to_broadcast([64, 8, 64]),
+            scalar1=-2.0, scalar2=0.0, op0=ALU.mult, op1=ALU.add,
+        )
+        sel = ident[64:128, 64:128].rearrange("p (q h m) -> p m q h", h=2, m=8)
+        nc.gpsimd.tensor_tensor(
+            out=dmat[64:128].rearrange("p m (q i) -> p m q i", q=4),
+            in0=sel[:, :, :, 0].unsqueeze(3).to_broadcast([64, 8, 4, 16]),
+            in1=sel[:, :, :, 1].unsqueeze(3).to_broadcast([64, 8, 4, 16]),
+            op=ALU.add,
+        )
+        g_f = const.tile([P, 8], F32, name="g_f")
+        nc.gpsimd.tensor_copy(out=g_f[:], in_=g_t[:])
+        gwq = const.tile([P, 8], F32, name="gwq")
+        nc.gpsimd.tensor_tensor(out=gwq[:], in0=g_t[:], in1=wq_t[:], op=ALU.mult)
+
+        kk = const.tile([P, 2, K], F32, name="kk")
+        kl = const.tile([P, 2, K], F32, name="kl")
+        neg_lc = const.tile([P, K], F32, name="neg_lc")
+        nc.vector.tensor_copy(out=kk[:, 0, :], in_=kv[:])
+        nc.vector.tensor_scalar(out=kk[:, 1, :], in0=kv[:], scalar1=-1.0, scalar2=float(K - 1), op0=ALU.mult, op1=ALU.add)
+        nc.vector.tensor_scalar_add(out=kk[:], in0=kk[:], scalar1=1e-6)
+        nc.scalar.activation(out=kl[:], in_=kk[:], func=ACT.Ln)
+        nc.vector.tensor_mul(out=kl[:], in0=kl[:], in1=kk[:])
+        nc.vector.scalar_tensor_tensor(
+            out=neg_lc[:], in0=kl[:, 0, :], scalar=(K - 1) * math.log(K - 1), in1=kl[:, 1, :], op0=ALU.subtract, op1=ALU.add
+        )
+
+        def perm_words(half):
+            for gg in range(2):
+                src = w1_raw[:, gg, 1024 * half : 1024 * half + 1024]
+                dst = w1_perm[:, gg, 1024 * half : 1024 * half + 1024]
+                nc.vector.tensor_copy(
+                    out=dst.rearrange("p (t m b) -> p t m b", t=4, b=2),
+                    in_=src.rearrange("p (m t b) -> p t m b", t=4, b=2),
+                )
+
+        def perm_scales():
+            for gg in range(2):
+                nc.vector.tensor_copy(
+                    out=s1_perm[:, gg, :].rearrange("p (f t m) -> p f t m", f=2, t=4),
+                    in_=s1_raw[:, gg, :].rearrange("p (f m t) -> p f t m", f=2, t=4),
+                )
+
+        def perm_head():
+            nc.vector.tensor_copy(
+                out=sh[:].rearrange("p g (h c n) -> p g h c n", h=2, c=2)[:, 0],
+                in_=sh_raw[:].rearrange("p g (c h n) -> p g h c n", h=2, c=2)[:, 0],
+            )
+            nc.vector.tensor_copy(
+                out=sh[:].rearrange("p g (h c n) -> p g h c n", h=2, c=2)[:, 1],
+                in_=sh_raw[:].rearrange("p g (c h n) -> p g h c n", h=2, c=2)[:, 1],
+            )
+
+        xq = {}
+        xc = {}
+        xs = {}
+        gl = {}
+        hb = {}
+        hz = {}
+        hc = {}
+        hs = {}
+        yab = {}
+        yt = {}
+        u_sb = {}
+        u_ps = {}
+        qh = {}
+        lg = {}
+        sums = {}
+
+        def widen(c, j):
+            if j == 0:
+                xq[c] = work.tile([P, 2, CH, 4], BF16, name="xq", align_bytes=64)
+            xw = work.tile([P, E], BF16, name="xw")
+            nc.vector.tensor_tensor(out=xw[:], in0=xb[:, c * TPC + j, :].bitcast(FP8), in1=scale[:], op=ALU.mult)
+            words = xw[:].bitcast(F32)
+            xt = psum.tile([P, 2, 2, P], F32, name="xt", tag="tr", bufs=3)
+            for gg in range(2):
+                for u in range(2):
+                    nc.tensor.transpose(xt[:, gg, u, :], words[:, 256 * gg + u : 256 * (gg + 1) : 2], ident[:])
+            dst = xq[c][:].rearrange("p g n t -> p (g n t)").bitcast(F32).rearrange("p (g n u) -> p g n u", g=2, u=2)
+            nc.scalar.copy(out=dst[:, :, j * P : (j + 1) * P, :], in_=xt[:].rearrange("p g u n -> p g n u"))
+
+        def quant_x(c):
+            xc[c] = work.tile([P, 2, CH], U32, name="xc", align_bytes=64, tag="m_codes", bufs=4)
+            xs[c] = work.tile([P, 2, CH], U8, name="xs", align_bytes=64)
+            for gg in range(2):
+                nc.vector.quantize_mx(
+                    out=xc[c][:, gg, :].bitcast(FP8X4), scales=xs[c][:, gg, :], in_=xq[c][:, gg].rearrange("p n t -> p (n t)")
+                )
+
+        def layer1(c, f):
+            gl[c, f] = work.tile([P, 4, CH], F32, name="gl", bufs=3)
+            for t in range(4):
+                blk = 4 * f + t
+                acc = psum.tile([P, CH], F32, name="acc", tag="s", bufs=5)
+                for gg in range(2):
+                    nc.tensor.matmul_mx(
+                        out=acc[:],
+                        lhsT=w1_perm[:, gg, 256 * blk : 256 * blk + 256].bitcast(FP4X4),
+                        lhsT_scale=s1_perm[:, gg, P * blk : P * blk + P],
+                        rhs=xc[c][:, gg, :].bitcast(FP8X4),
+                        rhs_scale=xs[c][:, gg, :],
+                        start=(gg == 0),
+                        stop=(gg == 1),
+                    )
+                nc.scalar.activation(out=gl[c, f][:, t, :], in_=acc[:], func=ACT.Gelu, bias=b1_t[:, blk : blk + 1])
+
+        def scale_h(c, f):
+            hz[c, f] = work.tile([P, 4, CH], BF16, name="hz", align_bytes=64, tag="m_hz")
+            for t in range(4):
+                blk = 4 * f + t
+                nc.scalar.activation(
+                    out=hz[c, f][:, t, :], in_=gl[c, f][:, t, :], func=ACT.Copy, scale=g_f[:, blk : blk + 1]
+                )
+
+        def weigh(c, f):
+            qh[c, f] = work.tile([P, 4, CH], F32, name="qh", bufs=4)
+            for t in range(4):
+                nc.gpsimd.tensor_scalar(
+                    out=qh[c, f][:, t, :], in0=gl[c, f][:, t, :], scalar1=gwq[:, 4 * f + t : 4 * f + t + 1], scalar2=0.0,
+                    op0=ALU.mult, op1=ALU.add,
+                )
+
+        def gain(c, f):
+            hb[c, f] = work.tile([P, CH, 4], BF16, name="hb", align_bytes=64, tag="m_hb")
+            if (c, f) in GAIN_S:
+                nc.vector.tensor_copy(out=hb[c, f][:], in_=hz[c, f][:].rearrange("p t n -> p n t"))
+                return
+            nc.vector.tensor_tensor(
+                out=hb[c, f][:],
+                in0=gl[c, f][:].rearrange("p t n -> p n t"),
+                in1=g_f[:, 4 * f : 4 * f + 4].unsqueeze(1).to_broadcast([P, CH, 4]),
+                op=ALU.mult,
+            )
+
+        def quant_h(c, f):
+            if f == 0:
+                hc[c] = work.tile([P, 2, CH], U32, name="hc", align_bytes=64, tag="m_codes", bufs=4)
+                hs[c] = work.tile([P, 2, CH], U8, name="hs", align_bytes=64)
+            nc.vector.quantize_mx(
+                out=hc[c][:, f, :].bitcast(FP8X4), scales=hs[c][:, f, :], in_=hb[c, f][:].rearrange("p n t -> p (n t)")
+            )
+
+        accs = {}
+
+        def relu(c, h):
+            nc.vector.tensor_scalar_max(out=yt[c][:, h, :], in0=accs[c, h][:], scalar1=0.0)
+
+        def layer2(c, late=False):
+            yab[c] = work.tile([P, 2, CH], F32, name="yab", bufs=4)
+            yt[c] = work.tile([P, 2, CH], F32, name="yt", bufs=4)
+            for h in range(2):
+                acc = psum.tile([P, CH], F32, name="acc", tag="s", bufs=5)
+                for f in range(2):
+                    nc.tensor.matmul_mx(
+                        out=acc[:],
+                        lhsT=wh[:, f, h, :].bitcast(FP4X4),
+                        lhsT_scale=sh[:, f, P * h : P * h + P],
+                        rhs=hc[c][:, f, :].bitcast(FP8X4),
+                        rhs_scale=hs[c][:, f, :],
+                        start=(f == 0),
+                        stop=(f == 1),
+                    )
+                nc.scalar.activation(out=yab[c][:, h, :], in_=acc[:], func=ACT.Abs)
+                accs[c, h] = acc
+                if not late:
+                    relu(c, h)
+
+        def logit_u(c):
+            u_ps[c] = psum.tile([P, TPC, P], F32, name="up", tag="tr", bufs=3)
+            for j in range(TPC):
+                for blk in range(8):
+                    nc.tensor.matmul(
+                        u_ps[c][:, j, :],
+                        lhsT=qh[c, blk // 4][:, blk % 4, j * P : (j + 1) * P],
+                        rhs=ident[:],
+                        start=(blk == 0),
+                        stop=(blk == 7),
+                        is_transpose=True,
+                    )
+
+        mx = {}
+
+        def logits(c):
+            u_sb[c] = work.tile([P, TPC], F32, name="u_sb", bufs=4)
+            nc.vector.tensor_reduce(out=u_sb[c][:], in_=u_ps[c][:], axis=AX.X, op=ALU.add)
+            lg[c] = work.tile([P, TPC, K], F32, name="lg", bufs=4)
+            mx[c] = work.tile([P, TPC], F32, name="mx", bufs=4)
+            for j in range(TPC):
+                nc.vector.scalar_tensor_tensor(
+                    out=lg[c][:, j, :], in0=kv[:], scalar=u_sb[c][:, j : j + 1], in1=neg_lc[:], op0=ALU.mult, op1=ALU.subtract
+                )
+            nc.vector.tensor_reduce(out=mx[c][:], in_=lg[c][:], axis=AX.X, op=ALU.max)
+            nc.vector.tensor_tensor(
+                out=lg[c][:], in0=lg[c][:], in1=mx[c][:].unsqueeze(2).to_broadcast([P, TPC, K]), op=ALU.subtract
+            )
+
+        def exps(c):
+            nc.scalar.activation(out=yab[c][:], in_=yab[c][:], func=ACT.Exp, scale=-1.0)
+
+        def softmax(c):
+            nc.scalar.activation(out=lg[c][:], in_=lg[c][:], func=ACT.Exp, scale=0.05)
+
+        def logs(c):
+            nc.scalar.activation(out=yab[c][:], in_=yab[c][:], func=ACT.Ln, bias=1.0)
+
+        def plus(c):
+            nc.vector.tensor_add(out=yt[c][:], in0=yt[c][:], in1=yab[c][:])
+
+        ytok = {}
+        d2 = {}
+        ee = {}
+        dl = {}
+        rs = {}
+
+        def turn(c):
+            ytok[c] = work.tile([P, TPC, 2, 2, 64], F32, name="ytok")
+            for jj in range(0, TPC, 2):
+                tr = psum.tile([P, 2, 2, 2, 64], F32, name="yp", tag="tr", bufs=3)
+                for j in range(2):
+                    for h in range(2):
+                        nc.tensor.transpose(
+                            tr[:, j, h].rearrange("p c n -> p (c n)"), yt[c][:, h, (jj + j) * P : (jj + j + 1) * P], ident[:]
+                        )
+                for j in range(2):
+                    nc.scalar.copy(out=ytok[c][:, jj + j].rearrange("p c h n -> p h c n"), in_=tr[:, j])
+
+        def pairs(c):
+            dl[c] = work.tile([P, TPC, 8, 8], F32, name="dl")
+            d2[c] = work.tile([P, TPC, 8, 8], F32, name="d2")
+            ee[c] = work.tile([P, TPC, 8, 8], F32, name="ee")
+            a = ytok[c][:, :, 1].rearrange("p j h (q s m) -> p j s m (h q)", s=2, m=8)
+            nc.vector.tensor_tensor(out=dl[c][:], in0=a[:, :, 0], in1=a[:, :, 1], op=ALU.subtract)
+            nc.vector.scalar_tensor_tensor(out=d2[c][:], in0=dl[c][:], scalar=2.0, in1=dl[c][:], op0=ALU.mult, op1=ALU.mult)
+            nc.vector.tensor_scalar(out=ee[c][:], in0=d2[c][:], scalar1=-0.25, scalar2=1.0, op0=ALU.mult, op1=ALU.add)
+            rs[c] = work.tile([P, TPC], F32, name="rs", bufs=4)
+            sums[c] = work.tile([P, TPC], F32, name="sums")
+            nc.vector.tensor_reduce(out=sums[c][:], in_=lg[c][:], axis=AX.X, op=ALU.add)
+            nc.vector.reciprocal(out=rs[c][:], in_=sums[c][:])
+
+        ss = {}
+        zz = {}
+        pp = {}
+        qq = {}
+        sp = {}
+        cp = {}
+        cs = {}
+
+        def st_s(i):
+            c, j = divmod(i, TPC)
+            for h in range(2):
+                if not (i == T // P - 1 and h == 1):
+                    ss[i, h] = psum.tile([P, 512], F32, name="s_ps", tag="s", bufs=5)
+                    nc.tensor.matmul(
+                        ss[i, h][:], lhsT=yt[c][:, h, j * P : (j + 1) * P], rhs=dmat[:].rearrange("p m n -> p (m n)"),
+                        start=True, stop=True,
+                    )
+
+        def st_z(i):
+            c, j = divmod(i, TPC)
+            zz[i] = work.tile([P, 8, 2, 64], F32, name="zz", align_bytes=64, tag="m_hb")
+            for h in range(2):
+                if i == T // P - 1 and h == 1:
+                    a = ytok[c][:, j, 1, h].rearrange("p (q s m) -> p s m q", s=2, m=8)
+                    asum = work.tile([P, 8, 4], F32, name="asum", bufs=1)
+                    nc.vector.tensor_tensor(out=asum[:], in0=a[:, 0], in1=a[:, 1], op=ALU.add)
+                    ss[i, h] = work.tile([P, 512], F32, name="s_sb", bufs=1)
+                    nc.vector.scalar_tensor_tensor(
+                        out=ss[i, h][:].rearrange("p (m q i) -> p m q i", m=8, q=4),
+                        in0=ytok[c][:, j, 0, h].rearrange("p (q i) -> p q i", q=4).unsqueeze(1).to_broadcast([P, 8, 4, 16]),
+                        scalar=-2.0,
+                        in1=asum[:].unsqueeze(3).to_broadcast([P, 8, 4, 16]),
+                        op0=ALU.mult, op1=ALU.add,
+                    )
+                nc.scalar.activation(
+                    out=zz[i][:, :, h, :], in_=ss[i, h][:].rearrange("p (m n) -> p m n", m=8), func=ACT.Square, scale=math.sqrt(0.5)
+                )
+
+        def st_den(i):
+            c, j = divmod(i, TPC)
+            q3 = qq[i][:].rearrange("p m h (q i) -> p (m h q) i", q=4)
+            nc.vector.tensor_tensor(
+                out=q3, in0=q3, in1=d2[c][:, j].rearrange("p m n -> p (m n)").unsqueeze(2).to_broadcast([P, 64, 16]), op=ALU.add
+            )
+            nc.scalar.activation(out=qq[i][:], in_=qq[i][:], func=ACT.Abs_reciprocal_sqrt)
+
+        def st_p(i):
+            c, j = divmod(i, TPC)
+            pp[i] = work.tile([P, 8, 2, 64], F32, name="pp", align_bytes=64, tag="m_hz")
+            qq[i] = work.tile([P, 8, 2, 64], F32, name="qq", bufs=3)
+            sp[i] = work.tile([P, 8, 2, 64], F32, name="sp", align_bytes=64, tag="m_codes", bufs=4)
+            nc.vector.tensor_tensor(
+                out=pp[i][:].rearrange("p m h (q i) -> p (m h q) i", q=4),
+                in0=zz[i][:].rearrange("p m h (q i) -> p (m h q) i", q=4),
+                in1=ee[c][:, j].rearrange("p m n -> p (m n)").unsqueeze(2).to_broadcast([P, 64, 16]),
+                op=ALU.add,
+            )
+            nc.scalar.activation(out=qq[i][:], in_=pp[i][:], func=ACT.Square)
+            for h in range(2):
+                nc.vector.scalar_tensor_tensor(
+                    out=sp[i][:, :, h, :], in0=ss[i, h][:].rearrange("p (m n) -> p m n", m=8), scalar=0.125,
+                    in1=pp[i][:, :, h, :], op0=ALU.mult, op1=ALU.mult,
+                )
+
+        def st_r(i):
+            nc.scalar.activation(out=qq[i][:], in_=qq[i][:], func=ACT.Square)
+
+        def st_f(i):
+            c, j = divmod(i, TPC)
+            nc.vector.tensor_mul(out=sp[i][:], in0=sp[i][:], in1=qq[i][:])
+
+        def st_sum(i):
+            c, j = divmod(i, TPC)
+            if j == 0:
+                cp[c] = psum.tile([P, TPC, P], F32, name="cp", tag="tr", bufs=3)
+            nc.tensor.matmul(
+                cp[c][:, j, :], lhsT=ytok[c][:, j, 0].rearrange("p h n -> p (h n)"), rhs=ident[:], start=True, stop=False,
+                is_transpose=True,
+            )
+            for m in range(8):
+                nc.tensor.matmul(
+                    cp[c][:, j, :], lhsT=sp[i][:, m].rearrange("p h n -> p (h n)"), rhs=ident[:], start=False, stop=(m == 7),
+                    is_transpose=True,
+                )
+
+        out_rows = out.rearrange("(c j p) k -> c p j k", p=P, j=TPC)
+
+        ot = {}
+        c2 = {}
+
+        def fin_copy(c, js):
+            if js[0] == 0:
+                cs[c] = work.tile([P, TPC, P], F32, name="cs")
+                c2[c] = psum.tile([P, TPC, P], F32, name="c2", tag="tr", bufs=3)
+                ot[c] = work.tile([P, TPC, K], F32, name="ot")
+            sl = slice(js[0], js[-1] + 1)
+            nc.scalar.activation(out=cs[c][:, sl, :], in_=cp[c][:, sl, :], func=ACT.Copy, scale=float(K))
+            for j in js:
+                nc.tensor.transpose(c2[c][:, j, :], cs[c][:, j, :], ident[:])
+
+        def fin_out(c, js):
+            sl = slice(js[0], js[-1] + 1)
+            for j in js:
+                nc.vector.scalar_tensor_tensor(
+                    out=ot[c][:, j, :], in0=lg[c][:, j, :], scalar=rs[c][:, j : j + 1], in1=c2[c][:, j, :],
+                    op0=ALU.mult, op1=ALU.mult,
+                )
+            nc.sync.dma_start(out=out_rows[c][:, sl, :], in_=ot[c][:, sl, :])
+
+        for j in range(TPC):
+            widen(0, j)
+        perm_words(0)
+        perm_scales()
+        widen(1, 0)
+        widen(1, 1)
+        for c in range(NCH + 1):
+            if c < NCH:
+                quant_x(c)
+                layer1(c, 0)
+                weigh(c, 0)
+            if c == 0:
+                perm_words(1)
+                perm_head()
+            if c + 1 < NCH:
+                widen(c + 1, 2)
+            if c > 0:
+                gain(c - 1, 1)
+            if c + 1 < NCH:
+                widen(c + 1, 3)
+            if c > 0:
+                quant_h(c - 1, 1)
+            if c < NCH:
+                gain(c, 0)
+            if c > 0 and c < NCH:
+                layer2(c - 1)
+            if c < NCH:
+                layer1(c, 1)
+                weigh(c, 1)
+            if c > 1:
+                logits(c - 2)
+            if c + 2 < NCH:
+                widen(c + 2, 0)
+            if c < NCH:
+                quant_h(c, 0)
+            if c + 2 < NCH:
+                widen(c + 2, 1)
+            if c == NCH:
+                layer2(c - 1)
+            if c > 0:
+                logit_u(c - 1)
+            if c < NCH:
+                scale_h(c, 1)
+            if c == NCH - 1:
+                for k in range(NCH - 1):
+                    exps(k)
+        softmax(0)
+        softmax(1)
+        exps(NCH - 1)
+        logits(NCH - 1)
+        softmax(2)
+        softmax(3)
+        logs(0)
+        plus(0)
+        logs(1)
+        turn(0)
+        st_s(0)
+        pairs(0)
+        logs(2)
+        st_z(0)
+        plus(1)
+        st_p(0)
+        st_s(1)
+        logs(3)
+        st_z(1)
+        plus(2)
+        st_s(2)
+        n = T // P
+        for i in range(-1, n + 1):
+            if 2 <= i + 3 < n:
+                st_z(i + 3)
+            if 0 <= i + 1 < n:
+                st_den(i + 1)
+            if 1 <= i + 2 < n:
+                st_p(i + 2)
+            if 0 <= i - 1:
+                st_sum(i - 1)
+            if 3 <= i + 4 < n:
+                st_s(i + 4)
+            if 0 <= i + 1 < n:
+                st_r(i + 1)
+            if 0 <= i < n:
+                st_f(i)
+            if i >= 1:
+                c, j = divmod(i - 1, TPC)
+                if j == 0:
+                    if c > 0:
+                        fin_copy(c - 1, range(TPC))
+                if j == 1 and c > 0:
+                    fin_out(c - 1, range(TPC))
+                if i == 2:
+                    plus(3)
+                if i == n - 1:
+                    fin_copy(c, range(2))
+                if i == n:
+                    fin_out(c, range(2))
+                    fin_copy(c, range(2, 4))
+                    fin_out(c, range(2, 4))
+            if 0 <= i < n and i % TPC == 0 and i // TPC + 1 < NCH:
+                turn(i // TPC + 1)
+            if 0 <= i < n and i % TPC == 1 and i // TPC + 1 < NCH:
+                pairs(i // TPC + 1)

@@ -34,7 +34,7 @@ def tile_attractordepthbinhead_w4_kernel(
         const = ctx.enter_context(tc.tile_pool(name="const", bufs=1))
         work = ctx.enter_context(tc.tile_pool(name="work", bufs=2))
         psum = ctx.enter_context(tc.psum_pool(name="psum", bufs=1))
-        ctx.enter_context(tc.manual_schedule())
+        ctx.enter_context(tc.manual_schedule(engines={mybir.EngineType.Activation}))
 
         w1_raw = const.tile([P, 2, 2048], U8, name="w1_raw", align_bytes=64)
         w1_perm = const.tile([P, 2, 2048], U8, name="w1_perm", align_bytes=64)

@@ -20,7 +20,9 @@ P = 128
 T, E, F, K = 2048, 1024, 1024, 128
 CH = 512
 NCH = T // CH
-GAIN_S = {(c, 1) for c in range(NCH)}
+GAIN_S = {(1, 1), (2, 1)}
+WEIGH_S = {(0, 0), (0, 1)}
+RELU_S = {0, 1, 2, 3}
 TPC = CH // P
 
 FLOPS = 2 * T * E * F + 2 * T * F * 2 * K
@@ -52,7 +54,8 @@ def tile_attractordepthbinhead_w4_kernel(
         nc.vector.memset(s1_raw[:].rearrange("p g n -> p (g n)").bitcast(I32), 0)
         nc.vector.memset(sh_raw[:].rearrange("p g n -> p (g n)").bitcast(I32), 0)
 
-        nc.scalar.dma_start(out=scale[:], in_=x_scale.rearrange("o k -> (o k)").partition_broadcast(P))
+        sc_col = const.tile([P, 8], F32, name="sc_col")
+        nc.sync.dma_start(out=sc_col[:], in_=x_scale.rearrange("o (c p) -> p (o c)", p=P))
 
         def load_w1(half):
             cols = slice(1024 * half, 1024 * half + 1024)
@@ -86,10 +89,10 @@ def tile_attractordepthbinhead_w4_kernel(
         for c in range(2, NCH):
             nc.sync.dma_start(out=xb[:, c * TPC : (c + 1) * TPC, :], in_=x_rows[:, c * TPC : (c + 1) * TPC, :])
 
-        ident = const.tile([P, P], F32, name="ident")
-        make_identity(nc, ident[:])
         kv = const.tile([P, K], F32, name="kv")
         nc.gpsimd.iota(kv[:], pattern=[[1, K]], base=0, channel_multiplier=0, allow_small_or_imprecise_dtypes=True)
+        ident = const.tile([P, P], F32, name="ident")
+        make_identity(nc, ident[:])
         dmat = const.tile([P, 8, 64], F32, name="dmat")
         nc.gpsimd.tensor_scalar(
             out=dmat[0:64],
@@ -119,6 +122,15 @@ def tile_attractordepthbinhead_w4_kernel(
         nc.vector.scalar_tensor_tensor(
             out=neg_lc[:], in0=kl[:, 0, :], scalar=(K - 1) * math.log(K - 1), in1=kl[:, 1, :], op0=ALU.subtract, op1=ALU.add
         )
+
+        warm = const.tile([P, 1], F32, name="warm")
+        nc.scalar.activation(out=warm[:], in_=kv[:, 0:1], func=ACT.Gelu)
+
+        for b in range(2):
+            sc_ps = psum.tile([P, 4, P], F32, name="sc_ps", tag="tr", bufs=3)
+            for c in range(4):
+                nc.tensor.transpose(sc_ps[:, c, :], sc_col[:, 4 * b + c : 4 * b + c + 1].to_broadcast([P, P]), ident[:])
+            nc.scalar.copy(out=scale[:, 512 * b : 512 * b + 512], in_=sc_ps[:].rearrange("p c n -> p (c n)"))
 
         def perm_words(half):
             for gg in range(2):
@@ -211,10 +223,11 @@ def tile_attractordepthbinhead_w4_kernel(
         def weigh(c, f):
             qh[c, f] = work.tile([P, 4, CH], F32, name="qh", bufs=4)
             for t in range(4):
-                nc.gpsimd.tensor_scalar(
-                    out=qh[c, f][:, t, :], in0=gl[c, f][:, t, :], scalar1=gwq[:, 4 * f + t : 4 * f + t + 1], scalar2=0.0,
-                    op0=ALU.mult, op1=ALU.add,
-                )
+                dst, src, v = qh[c, f][:, t, :], gl[c, f][:, t, :], gwq[:, 4 * f + t : 4 * f + t + 1]
+                if (c, f) in WEIGH_S:
+                    nc.scalar.activation(out=dst, in_=src, func=ACT.Copy, scale=v)
+                else:
+                    nc.vector.tensor_scalar(out=dst, in0=src, scalar1=v, scalar2=0.0, op0=ALU.mult, op1=ALU.add)
 
         def gain(c, f):
             hb[c, f] = work.tile([P, CH, 4], BF16, name="hb", align_bytes=64, tag="m_hb")
@@ -236,12 +249,7 @@ def tile_attractordepthbinhead_w4_kernel(
                 out=hc[c][:, f, :].bitcast(FP8X4), scales=hs[c][:, f, :], in_=hb[c, f][:].rearrange("p n t -> p (n t)")
             )
 
-        accs = {}
-
-        def relu(c, h):
-            nc.vector.tensor_scalar_max(out=yt[c][:, h, :], in0=accs[c, h][:], scalar1=0.0)
-
-        def layer2(c, late=False):
+        def layer2(c):
             yab[c] = work.tile([P, 2, CH], F32, name="yab", bufs=4)
             yt[c] = work.tile([P, 2, CH], F32, name="yt", bufs=4)
             for h in range(2):
@@ -257,9 +265,10 @@ def tile_attractordepthbinhead_w4_kernel(
                         stop=(f == 1),
                     )
                 nc.scalar.activation(out=yab[c][:, h, :], in_=acc[:], func=ACT.Abs)
-                accs[c, h] = acc
-                if not late:
-                    relu(c, h)
+                if c in RELU_S:
+                    nc.scalar.activation(out=yt[c][:, h, :], in_=acc[:], func=ACT.Relu)
+                else:
+                    nc.vector.tensor_scalar_max(out=yt[c][:, h, :], in0=acc[:], scalar1=0.0)
 
         def logit_u(c):
             u_ps[c] = psum.tile([P, TPC, P], F32, name="up", tag="tr", bufs=3)
@@ -308,17 +317,26 @@ def tile_attractordepthbinhead_w4_kernel(
         dl = {}
         rs = {}
 
-        def turn(c):
-            ytok[c] = work.tile([P, TPC, 2, 2, 64], F32, name="ytok")
+        yp = {}
+
+        def turn_pe(c):
             for jj in range(0, TPC, 2):
-                tr = psum.tile([P, 2, 2, 2, 64], F32, name="yp", tag="tr", bufs=3)
+                yp[c, jj] = psum.tile([P, 2, 2, 2, 64], F32, name="yp", tag="tr", bufs=3)
                 for j in range(2):
                     for h in range(2):
                         nc.tensor.transpose(
-                            tr[:, j, h].rearrange("p c n -> p (c n)"), yt[c][:, h, (jj + j) * P : (jj + j + 1) * P], ident[:]
+                            yp[c, jj][:, j, h].rearrange("p c n -> p (c n)"), yt[c][:, h, (jj + j) * P : (jj + j + 1) * P], ident[:]
                         )
+
+        def turn_copy(c):
+            ytok[c] = work.tile([P, TPC, 2, 2, 64], F32, name="ytok")
+            for jj in range(0, TPC, 2):
                 for j in range(2):
-                    nc.scalar.copy(out=ytok[c][:, jj + j].rearrange("p c h n -> p h c n"), in_=tr[:, j])
+                    nc.scalar.copy(out=ytok[c][:, jj + j].rearrange("p c h n -> p h c n"), in_=yp[c, jj][:, j])
+
+        def turn(c):
+            turn_pe(c)
+            turn_copy(c)
 
         def pairs(c):
             dl[c] = work.tile([P, TPC, 8, 8], F32, name="dl")
@@ -391,6 +409,8 @@ def tile_attractordepthbinhead_w4_kernel(
                 op=ALU.add,
             )
             nc.scalar.activation(out=qq[i][:], in_=pp[i][:], func=ACT.Square)
+
+        def st_sp(i):
             for h in range(2):
                 nc.vector.scalar_tensor_tensor(
                     out=sp[i][:, :, h, :], in0=ss[i, h][:].rearrange("p (m n) -> p m n", m=8), scalar=0.125,
@@ -452,6 +472,8 @@ def tile_attractordepthbinhead_w4_kernel(
             if c < NCH:
                 quant_x(c)
                 layer1(c, 0)
+                if (c, 0) in GAIN_S:
+                    scale_h(c, 0)
                 weigh(c, 0)
             if c == 0:
                 perm_words(1)
@@ -483,7 +505,7 @@ def tile_attractordepthbinhead_w4_kernel(
                 layer2(c - 1)
             if c > 0:
                 logit_u(c - 1)
-            if c < NCH:
+            if c < NCH and (c, 1) in GAIN_S:
                 scale_h(c, 1)
             if c == NCH - 1:
                 for k in range(NCH - 1):
@@ -497,26 +519,30 @@ def tile_attractordepthbinhead_w4_kernel(
         logs(0)
         plus(0)
         logs(1)
-        turn(0)
+        turn_pe(0)
         st_s(0)
-        pairs(0)
         logs(2)
+        turn_copy(0)
         st_z(0)
+        pairs(0)
         plus(1)
-        st_p(0)
-        st_s(1)
         logs(3)
+        st_s(1)
         st_z(1)
+        st_p(0)
+        st_sp(0)
         plus(2)
         st_s(2)
         n = T // P
         for i in range(-1, n + 1):
             if 2 <= i + 3 < n:
                 st_z(i + 3)
+            if 1 <= i + 2 < n:
+                st_p(i + 2)
             if 0 <= i + 1 < n:
                 st_den(i + 1)
             if 1 <= i + 2 < n:
-                st_p(i + 2)
+                st_sp(i + 2)
             if 0 <= i - 1:
                 st_sum(i - 1)
             if 3 <= i + 4 < n:
@@ -532,14 +558,14 @@ def tile_attractordepthbinhead_w4_kernel(
                         fin_copy(c - 1, range(TPC))
                 if j == 1 and c > 0:
                     fin_out(c - 1, range(TPC))
-                if i == 2:
-                    plus(3)
                 if i == n - 1:
                     fin_copy(c, range(2))
                 if i == n:
                     fin_out(c, range(2))
                     fin_copy(c, range(2, 4))
                     fin_out(c, range(2, 4))
+            if i == 2:
+                plus(3)
             if 0 <= i < n and i % TPC == 0 and i // TPC + 1 < NCH:
                 turn(i // TPC + 1)
             if 0 <= i < n and i % TPC == 1 and i // TPC + 1 < NCH:

@@ -99,6 +99,10 @@ def tile_attractordepthbinhead_w4_kernel(
             in0=ident[0:64, 0:64].unsqueeze(1).to_broadcast([64, 8, 64]),
             scalar1=-2.0, scalar2=0.0, op0=ALU.mult, op1=ALU.add,
         )
+        pick = const.tile([P, 2, P], F32, name="pick")
+        nc.gpsimd.memset(pick[:], 0.0)
+        for h in range(2):
+            nc.gpsimd.tensor_copy(out=pick[:, h, 0:64], in_=ident[:, 64 * h : 64 * h + 64])
         sel = ident[64:128, 64:128].rearrange("p (q h m) -> p m q h", h=2, m=8)
         nc.gpsimd.tensor_tensor(
             out=dmat[64:128].rearrange("p m (q i) -> p m q i", q=4),
@@ -232,12 +236,15 @@ def tile_attractordepthbinhead_w4_kernel(
         def gain(c, f):
             hb[c, f] = work.tile([P, CH, 4], BF16, name="hb", align_bytes=64, tag="m_hb")
             if (c, f) in GAIN_S:
-                nc.vector.tensor_copy(out=hb[c, f][:], in_=hz[c, f][:].rearrange("p t n -> p n t"))
+                nc.vector.tensor_copy(
+                    out=hb[c, f][:].rearrange("p (n i) t -> p n t i", i=4),
+                    in_=hz[c, f][:].rearrange("p t (n i) -> p n t i", i=4),
+                )
                 return
             nc.vector.tensor_tensor(
-                out=hb[c, f][:],
-                in0=gl[c, f][:].rearrange("p t n -> p n t"),
-                in1=g_f[:, 4 * f : 4 * f + 4].unsqueeze(1).to_broadcast([P, CH, 4]),
+                out=hb[c, f][:].rearrange("p (n i) t -> p n t i", i=4),
+                in0=gl[c, f][:].rearrange("p t (n i) -> p n t i", i=4),
+                in1=g_f[:, 4 * f : 4 * f + 4].unsqueeze(1).unsqueeze(3).to_broadcast([P, CH // 4, 4, 4]),
                 op=ALU.mult,
             )
 
@@ -321,18 +328,19 @@ def tile_attractordepthbinhead_w4_kernel(
 
         def turn_pe(c):
             for jj in range(0, TPC, 2):
-                yp[c, jj] = psum.tile([P, 2, 2, 2, 64], F32, name="yp", tag="tr", bufs=3)
-                for j in range(2):
-                    for h in range(2):
-                        nc.tensor.transpose(
-                            yp[c, jj][:, j, h].rearrange("p c n -> p (c n)"), yt[c][:, h, (jj + j) * P : (jj + j + 1) * P], ident[:]
-                        )
+                yp[c, jj] = psum.tile([P, 4, 2, 64], F32, name="yp", tag="tr", bufs=3)
+                for b in range(4):
+                    j, h = jj + b // 2, b % 2
+                    nc.tensor.transpose(
+                        yp[c, jj][:, b].rearrange("p c n -> p (c n)"), yt[c][:, h, j * P : (j + 1) * P], ident[:]
+                    )
 
         def turn_copy(c):
-            ytok[c] = work.tile([P, TPC, 2, 2, 64], F32, name="ytok")
+            ytok[c] = work.tile([P, TPC, 2, 64], F32, name="ytok")
             for jj in range(0, TPC, 2):
-                for j in range(2):
-                    nc.scalar.copy(out=ytok[c][:, jj + j].rearrange("p c h n -> p h c n"), in_=yp[c, jj][:, j])
+                nc.scalar.copy(
+                    out=ytok[c][:, jj : jj + 2].rearrange("p j h n -> p (j h) n"), in_=yp[c, jj][:, :, 1]
+                )
 
         def turn(c):
             turn_pe(c)
@@ -342,13 +350,14 @@ def tile_attractordepthbinhead_w4_kernel(
             dl[c] = work.tile([P, TPC, 8, 8], F32, name="dl")
             d2[c] = work.tile([P, TPC, 8, 8], F32, name="d2")
             ee[c] = work.tile([P, TPC, 8, 8], F32, name="ee")
-            a = ytok[c][:, :, 1].rearrange("p j h (q s m) -> p j s m (h q)", s=2, m=8)
+            a = ytok[c][:].rearrange("p j h (q s m) -> p j s m (h q)", s=2, m=8)
             nc.vector.tensor_tensor(out=dl[c][:], in0=a[:, :, 0], in1=a[:, :, 1], op=ALU.subtract)
             nc.vector.scalar_tensor_tensor(out=d2[c][:], in0=dl[c][:], scalar=2.0, in1=dl[c][:], op0=ALU.mult, op1=ALU.mult)
             nc.vector.tensor_scalar(out=ee[c][:], in0=d2[c][:], scalar1=-0.25, scalar2=1.0, op0=ALU.mult, op1=ALU.add)
             rs[c] = work.tile([P, TPC], F32, name="rs", bufs=4)
             sums[c] = work.tile([P, TPC], F32, name="sums")
             nc.vector.tensor_reduce(out=sums[c][:], in_=lg[c][:], axis=AX.X, op=ALU.add)
+            nc.vector.tensor_scalar_mul(out=sums[c][:], in0=sums[c][:], scalar1=1.0 / K)
             nc.vector.reciprocal(out=rs[c][:], in_=sums[c][:])
 
         ss = {}
@@ -362,29 +371,16 @@ def tile_attractordepthbinhead_w4_kernel(
         def st_s(i):
             c, j = divmod(i, TPC)
             for h in range(2):
-                if not (i == T // P - 1 and h == 1):
-                    ss[i, h] = psum.tile([P, 512], F32, name="s_ps", tag="s", bufs=5)
-                    nc.tensor.matmul(
-                        ss[i, h][:], lhsT=yt[c][:, h, j * P : (j + 1) * P], rhs=dmat[:].rearrange("p m n -> p (m n)"),
-                        start=True, stop=True,
-                    )
+                ss[i, h] = psum.tile([P, 512], F32, name="s_ps", tag="s", bufs=5)
+                nc.tensor.matmul(
+                    ss[i, h][:], lhsT=yt[c][:, h, j * P : (j + 1) * P], rhs=dmat[:].rearrange("p m n -> p (m n)"),
+                    start=True, stop=True,
+                )
 
-        def st_z(i):
-            c, j = divmod(i, TPC)
-            zz[i] = work.tile([P, 8, 2, 64], F32, name="zz", align_bytes=64, tag="m_hb")
-            for h in range(2):
-                if i == T // P - 1 and h == 1:
-                    a = ytok[c][:, j, 1, h].rearrange("p (q s m) -> p s m q", s=2, m=8)
-                    asum = work.tile([P, 8, 4], F32, name="asum", bufs=1)
-                    nc.vector.tensor_tensor(out=asum[:], in0=a[:, 0], in1=a[:, 1], op=ALU.add)
-                    ss[i, h] = work.tile([P, 512], F32, name="s_sb", bufs=1)
-                    nc.vector.scalar_tensor_tensor(
-                        out=ss[i, h][:].rearrange("p (m q i) -> p m q i", m=8, q=4),
-                        in0=ytok[c][:, j, 0, h].rearrange("p (q i) -> p q i", q=4).unsqueeze(1).to_broadcast([P, 8, 4, 16]),
-                        scalar=-2.0,
-                        in1=asum[:].unsqueeze(3).to_broadcast([P, 8, 4, 16]),
-                        op0=ALU.mult, op1=ALU.add,
-                    )
+        def st_z(i, halves=(0, 1)):
+            if halves[0] == 0:
+                zz[i] = work.tile([P, 8, 2, 64], F32, name="zz", align_bytes=64, tag="m_hb")
+            for h in halves:
                 nc.scalar.activation(
                     out=zz[i][:, :, h, :], in_=ss[i, h][:].rearrange("p (m n) -> p m n", m=8), func=ACT.Square, scale=math.sqrt(0.5)
                 )
@@ -428,13 +424,9 @@ def tile_attractordepthbinhead_w4_kernel(
             c, j = divmod(i, TPC)
             if j == 0:
                 cp[c] = psum.tile([P, TPC, P], F32, name="cp", tag="tr", bufs=3)
-            nc.tensor.matmul(
-                cp[c][:, j, :], lhsT=ytok[c][:, j, 0].rearrange("p h n -> p (h n)"), rhs=ident[:], start=True, stop=False,
-                is_transpose=True,
-            )
             for m in range(8):
                 nc.tensor.matmul(
-                    cp[c][:, j, :], lhsT=sp[i][:, m].rearrange("p h n -> p (h n)"), rhs=ident[:], start=False, stop=(m == 7),
+                    cp[c][:, j, :], lhsT=sp[i][:, m].rearrange("p h n -> p (h n)"), rhs=ident[:], start=(m == 0), stop=(m == 7),
                     is_transpose=True,
                 )
 
@@ -446,19 +438,25 @@ def tile_attractordepthbinhead_w4_kernel(
         def fin_copy(c, js):
             if js[0] == 0:
                 cs[c] = work.tile([P, TPC, P], F32, name="cs")
-                c2[c] = psum.tile([P, TPC, P], F32, name="c2", tag="tr", bufs=3)
                 ot[c] = work.tile([P, TPC, K], F32, name="ot")
             sl = slice(js[0], js[-1] + 1)
-            nc.scalar.activation(out=cs[c][:, sl, :], in_=cp[c][:, sl, :], func=ACT.Copy, scale=float(K))
+            nc.scalar.copy(out=cs[c][:, sl, :], in_=cp[c][:, sl, :])
             for j in js:
-                nc.tensor.transpose(c2[c][:, j, :], cs[c][:, j, :], ident[:])
+                if j % 2 == 0:
+                    c2[c, j // 2] = psum.tile([P, 2, 2, P], F32, name="c2", tag="tr", bufs=3)
+                for h in range(2):
+                    dst = c2[c, j // 2][:, j % 2, h, :]
+                    nc.tensor.matmul(dst, lhsT=cs[c][:, j, :], rhs=pick[:, h, :], start=True, stop=False, is_transpose=True)
+                    nc.tensor.matmul(
+                        dst, lhsT=yt[c][:, h, j * P : (j + 1) * P], rhs=ident[:], start=False, stop=True, is_transpose=True
+                    )
 
         def fin_out(c, js):
             sl = slice(js[0], js[-1] + 1)
             for j in js:
                 nc.vector.scalar_tensor_tensor(
-                    out=ot[c][:, j, :], in0=lg[c][:, j, :], scalar=rs[c][:, j : j + 1], in1=c2[c][:, j, :],
-                    op0=ALU.mult, op1=ALU.mult,
+                    out=ot[c][:, j, :].rearrange("p (h n) -> p h n", h=2), in0=lg[c][:, j, :].rearrange("p (h n) -> p h n", h=2), scalar=rs[c][:, j : j + 1],
+                    in1=c2[c, j // 2][:, j % 2, :, 0:64], op0=ALU.mult, op1=ALU.mult,
                 )
             nc.sync.dma_start(out=out_rows[c][:, sl, :], in_=ot[c][:, sl, :])
 
@@ -536,11 +534,13 @@ def tile_attractordepthbinhead_w4_kernel(
         n = T // P
         for i in range(-1, n + 1):
             if 2 <= i + 3 < n:
-                st_z(i + 3)
+                st_z(i + 3, (0,))
             if 1 <= i + 2 < n:
                 st_p(i + 2)
             if 0 <= i + 1 < n:
                 st_den(i + 1)
+            if 2 <= i + 3 < n:
+                st_z(i + 3, (1,))
             if 1 <= i + 2 < n:
                 st_sp(i + 2)
             if 0 <= i - 1:

@@ -20,9 +20,10 @@ P = 128
 T, E, F, K = 2048, 1024, 1024, 128
 CH = 512
 NCH = T // CH
-GAIN_S = {(1, 1), (2, 1)}
+SPLIT = {T // P - 1}
+GAIN_S = {(1, 1)}
 WEIGH_S = {(0, 0), (0, 1)}
-RELU_S = {0, 1, 2, 3}
+RELU_S = {0, 1}
 TPC = CH // P
 
 FLOPS = 2 * T * E * F + 2 * T * F * 2 * K
@@ -114,6 +115,7 @@ def tile_attractordepthbinhead_w4_kernel(
         nc.gpsimd.tensor_copy(out=g_f[:], in_=g_t[:])
         gwq = const.tile([P, 8], F32, name="gwq")
         nc.gpsimd.tensor_tensor(out=gwq[:], in0=g_t[:], in1=wq_t[:], op=ALU.mult)
+        nc.gpsimd.tensor_scalar(out=gwq[:], in0=gwq[:], scalar1=0.05, scalar2=0.0, op0=ALU.mult, op1=ALU.add)
 
         kk = const.tile([P, 2, K], F32, name="kk")
         kl = const.tile([P, 2, K], F32, name="kl")
@@ -176,7 +178,9 @@ def tile_attractordepthbinhead_w4_kernel(
         u_ps = {}
         qh = {}
         lg = {}
-        sums = {}
+        shift = {}
+        rs = {}
+        weight = const.tile([P, K], F32, name="weight")
 
         def widen(c, j):
             if j == 0:
@@ -290,27 +294,39 @@ def tile_attractordepthbinhead_w4_kernel(
                         is_transpose=True,
                     )
 
-        mx = {}
 
         def logits(c):
             u_sb[c] = work.tile([P, TPC], F32, name="u_sb", bufs=4)
+            shift[c] = work.tile([P, TPC], F32, name="shift", bufs=4)
             nc.vector.tensor_reduce(out=u_sb[c][:], in_=u_ps[c][:], axis=AX.X, op=ALU.add)
-            lg[c] = work.tile([P, TPC, K], F32, name="lg", bufs=4)
-            mx[c] = work.tile([P, TPC], F32, name="mx", bufs=4)
-            for j in range(TPC):
-                nc.vector.scalar_tensor_tensor(
-                    out=lg[c][:, j, :], in0=kv[:], scalar=u_sb[c][:, j : j + 1], in1=neg_lc[:], op0=ALU.mult, op1=ALU.subtract
-                )
-            nc.vector.tensor_reduce(out=mx[c][:], in_=lg[c][:], axis=AX.X, op=ALU.max)
-            nc.vector.tensor_tensor(
-                out=lg[c][:], in0=lg[c][:], in1=mx[c][:].unsqueeze(2).to_broadcast([P, TPC, K]), op=ALU.subtract
+            nc.vector.tensor_scalar(
+                out=shift[c][:], in0=u_sb[c][:], scalar1=-float(K - 1), scalar2=0.0, op0=ALU.mult, op1=ALU.min
             )
+
+        def weights():
+            nc.scalar.activation(out=weight[:], in_=neg_lc[:], func=ACT.Exp, scale=-0.05)
+
+        def softmax(c):
+            if c % 2 == 0:
+                lg[c // 2] = work.tile([P, 2 * TPC, K], F32, name="lg")
+            for j in range(TPC):
+                nc.scalar.activation(
+                    out=lg[c // 2][:, c % 2 * TPC + j, :], in_=kv[:], func=ACT.Exp,
+                    scale=u_sb[c][:, j : j + 1], bias=shift[c][:, j : j + 1],
+                )
+
+        def recips(d):
+            sums = work.tile([P, 2 * TPC], F32, name="sums")
+            rs[d] = work.tile([P, 2 * TPC], F32, name="rs")
+            nc.vector.tensor_tensor(
+                out=lg[d][:], in0=lg[d][:], in1=weight[:].unsqueeze(1).to_broadcast([P, 2 * TPC, K]), op=ALU.mult
+            )
+            nc.vector.tensor_reduce(out=sums[:], in_=lg[d][:], axis=AX.X, op=ALU.add)
+            nc.vector.tensor_scalar_mul(out=sums[:], in0=sums[:], scalar1=1.0 / K)
+            nc.vector.reciprocal(out=rs[d][:], in_=sums[:])
 
         def exps(c):
             nc.scalar.activation(out=yab[c][:], in_=yab[c][:], func=ACT.Exp, scale=-1.0)
-
-        def softmax(c):
-            nc.scalar.activation(out=lg[c][:], in_=lg[c][:], func=ACT.Exp, scale=0.05)
 
         def logs(c):
             nc.scalar.activation(out=yab[c][:], in_=yab[c][:], func=ACT.Ln, bias=1.0)
@@ -322,7 +338,6 @@ def tile_attractordepthbinhead_w4_kernel(
         d2 = {}
         ee = {}
         dl = {}
-        rs = {}
 
         yp = {}
 
@@ -346,19 +361,18 @@ def tile_attractordepthbinhead_w4_kernel(
             turn_pe(c)
             turn_copy(c)
 
-        def pairs(c):
+        def pair_delta(c):
             dl[c] = work.tile([P, TPC, 8, 8], F32, name="dl")
-            d2[c] = work.tile([P, TPC, 8, 8], F32, name="d2")
-            ee[c] = work.tile([P, TPC, 8, 8], F32, name="ee")
             a = ytok[c][:].rearrange("p j h (q s m) -> p j s m (h q)", s=2, m=8)
             nc.vector.tensor_tensor(out=dl[c][:], in0=a[:, :, 0], in1=a[:, :, 1], op=ALU.subtract)
+
+        def pair_d2(c):
+            d2[c] = work.tile([P, TPC, 8, 8], F32, name="d2")
             nc.vector.scalar_tensor_tensor(out=d2[c][:], in0=dl[c][:], scalar=2.0, in1=dl[c][:], op0=ALU.mult, op1=ALU.mult)
+
+        def pair_e(c):
+            ee[c] = work.tile([P, TPC, 8, 8], F32, name="ee")
             nc.vector.tensor_scalar(out=ee[c][:], in0=d2[c][:], scalar1=-0.25, scalar2=1.0, op0=ALU.mult, op1=ALU.add)
-            rs[c] = work.tile([P, TPC], F32, name="rs", bufs=4)
-            sums[c] = work.tile([P, TPC], F32, name="sums")
-            nc.vector.tensor_reduce(out=sums[c][:], in_=lg[c][:], axis=AX.X, op=ALU.add)
-            nc.vector.tensor_scalar_mul(out=sums[c][:], in0=sums[c][:], scalar1=1.0 / K)
-            nc.vector.reciprocal(out=rs[c][:], in_=sums[c][:])
 
         ss = {}
         zz = {}
@@ -385,26 +399,33 @@ def tile_attractordepthbinhead_w4_kernel(
                     out=zz[i][:, :, h, :], in_=ss[i, h][:].rearrange("p (m n) -> p m n", m=8), func=ACT.Square, scale=math.sqrt(0.5)
                 )
 
+        def parts(i):
+            return [slice(0, 4), slice(4, 8)] if i in SPLIT else [slice(0, 8)]
+
+        def rows(ap):
+            return ap.rearrange("p m h (q i) -> p (m h q) i", q=4)
+
+        def spread(ap):
+            w = ap.rearrange("p m n -> p (m n)")
+            return w.unsqueeze(2).to_broadcast([P, w.shape[1], 16])
+
         def st_den(i):
             c, j = divmod(i, TPC)
-            q3 = qq[i][:].rearrange("p m h (q i) -> p (m h q) i", q=4)
-            nc.vector.tensor_tensor(
-                out=q3, in0=q3, in1=d2[c][:, j].rearrange("p m n -> p (m n)").unsqueeze(2).to_broadcast([P, 64, 16]), op=ALU.add
-            )
-            nc.scalar.activation(out=qq[i][:], in_=qq[i][:], func=ACT.Abs_reciprocal_sqrt)
+            for m in parts(i):
+                q3 = rows(qq[i][:, m])
+                nc.vector.tensor_tensor(out=q3, in0=q3, in1=spread(d2[c][:, j, m]), op=ALU.add)
+                nc.scalar.activation(out=qq[i][:, m], in_=qq[i][:, m], func=ACT.Abs_reciprocal_sqrt)
 
         def st_p(i):
             c, j = divmod(i, TPC)
             pp[i] = work.tile([P, 8, 2, 64], F32, name="pp", align_bytes=64, tag="m_hz")
             qq[i] = work.tile([P, 8, 2, 64], F32, name="qq", bufs=3)
             sp[i] = work.tile([P, 8, 2, 64], F32, name="sp", align_bytes=64, tag="m_codes", bufs=4)
-            nc.vector.tensor_tensor(
-                out=pp[i][:].rearrange("p m h (q i) -> p (m h q) i", q=4),
-                in0=zz[i][:].rearrange("p m h (q i) -> p (m h q) i", q=4),
-                in1=ee[c][:, j].rearrange("p m n -> p (m n)").unsqueeze(2).to_broadcast([P, 64, 16]),
-                op=ALU.add,
-            )
-            nc.scalar.activation(out=qq[i][:], in_=pp[i][:], func=ACT.Square)
+            for m in parts(i):
+                nc.vector.tensor_tensor(
+                    out=rows(pp[i][:, m]), in0=rows(zz[i][:, m]), in1=spread(ee[c][:, j, m]), op=ALU.add
+                )
+                nc.scalar.activation(out=qq[i][:, m], in_=pp[i][:, m], func=ACT.Square)
 
         def st_sp(i):
             for h in range(2):
@@ -414,11 +435,12 @@ def tile_attractordepthbinhead_w4_kernel(
                 )
 
         def st_r(i):
-            nc.scalar.activation(out=qq[i][:], in_=qq[i][:], func=ACT.Square)
+            for m in parts(i):
+                nc.scalar.activation(out=qq[i][:, m], in_=qq[i][:, m], func=ACT.Square)
 
         def st_f(i):
-            c, j = divmod(i, TPC)
-            nc.vector.tensor_mul(out=sp[i][:], in0=sp[i][:], in1=qq[i][:])
+            for m in parts(i):
+                nc.vector.tensor_mul(out=sp[i][:, m], in0=sp[i][:, m], in1=qq[i][:, m])
 
         def st_sum(i):
             c, j = divmod(i, TPC)
@@ -455,65 +477,72 @@ def tile_attractordepthbinhead_w4_kernel(
             sl = slice(js[0], js[-1] + 1)
             for j in js:
                 nc.vector.scalar_tensor_tensor(
-                    out=ot[c][:, j, :].rearrange("p (h n) -> p h n", h=2), in0=lg[c][:, j, :].rearrange("p (h n) -> p h n", h=2), scalar=rs[c][:, j : j + 1],
+                    out=ot[c][:, j, :].rearrange("p (h n) -> p h n", h=2), in0=lg[c // 2][:, c % 2 * TPC + j, :].rearrange("p (h n) -> p h n", h=2),
+                    scalar=rs[c // 2][:, c % 2 * TPC + j : c % 2 * TPC + j + 1],
                     in1=c2[c, j // 2][:, j % 2, :, 0:64], op0=ALU.mult, op1=ALU.mult,
                 )
             nc.sync.dma_start(out=out_rows[c][:, sl, :], in_=ot[c][:, sl, :])
 
         for j in range(TPC):
             widen(0, j)
-        perm_words(0)
         perm_scales()
         widen(1, 0)
         widen(1, 1)
-        for c in range(NCH + 1):
-            if c < NCH:
-                quant_x(c)
-                layer1(c, 0)
-                if (c, 0) in GAIN_S:
-                    scale_h(c, 0)
-                weigh(c, 0)
+        perm_words(0)
+        widen(1, 2)
+        for c in range(NCH):
+            quant_x(c)
+            if c > 1:
+                logit_u(c - 2)
+            if c > 2:
+                logits(c - 3)
+            if (c - 1, 1) in GAIN_S:
+                scale_h(c - 1, 1)
+            if c > 0 and (c - 1, 1) not in GAIN_S:
+                gain(c - 1, 1)
+            layer1(c, 0)
+            weigh(c, 0)
             if c == 0:
                 perm_words(1)
-                perm_head()
-            if c + 1 < NCH:
-                widen(c + 1, 2)
-            if c > 0:
-                gain(c - 1, 1)
             if c + 1 < NCH:
                 widen(c + 1, 3)
+            if (c - 1, 1) in GAIN_S:
+                gain(c - 1, 1)
             if c > 0:
                 quant_h(c - 1, 1)
-            if c < NCH:
-                gain(c, 0)
-            if c > 0 and c < NCH:
-                layer2(c - 1)
-            if c < NCH:
-                layer1(c, 1)
-                weigh(c, 1)
-            if c > 1:
-                logits(c - 2)
+            gain(c, 0)
+            if c == 0:
+                perm_head()
+            if c == 1:
+                layer2(0)
             if c + 2 < NCH:
                 widen(c + 2, 0)
-            if c < NCH:
-                quant_h(c, 0)
-            if c + 2 < NCH:
                 widen(c + 2, 1)
-            if c == NCH:
-                layer2(c - 1)
-            if c > 0:
-                logit_u(c - 1)
-            if c < NCH and (c, 1) in GAIN_S:
-                scale_h(c, 1)
-            if c == NCH - 1:
-                for k in range(NCH - 1):
-                    exps(k)
+            layer1(c, 1)
+            if c == 2:
+                layer2(1)
+            weigh(c, 1)
+            quant_h(c, 0)
+            if c + 2 < NCH:
+                widen(c + 2, 2)
+        weights()
+        logits(NCH - 3)
+        logit_u(NCH - 2)
+        exps(0)
+        exps(1)
+        logit_u(NCH - 1)
+        layer2(NCH - 2)
+        logits(NCH - 2)
         softmax(0)
-        softmax(1)
-        exps(NCH - 1)
         logits(NCH - 1)
+        gain(NCH - 1, 1)
+        exps(NCH - 2)
+        quant_h(NCH - 1, 1)
+        softmax(1)
         softmax(2)
+        layer2(NCH - 1)
         softmax(3)
+        exps(NCH - 1)
         logs(0)
         plus(0)
         logs(1)
@@ -521,28 +550,39 @@ def tile_attractordepthbinhead_w4_kernel(
         st_s(0)
         logs(2)
         turn_copy(0)
-        st_z(0)
-        pairs(0)
+        pair_delta(0)
         plus(1)
+        pair_d2(0)
         logs(3)
         st_s(1)
+        st_z(0)
+        recips(0)
+        pair_e(0)
         st_z(1)
         st_p(0)
-        st_sp(0)
         plus(2)
+        st_sp(0)
+        recips(1)
         st_s(2)
         n = T // P
         for i in range(-1, n + 1):
+            nxt = i // TPC + 1 if 0 <= i < n and i % TPC == 1 and i // TPC + 1 < NCH else 0
             if 2 <= i + 3 < n:
                 st_z(i + 3, (0,))
             if 1 <= i + 2 < n:
                 st_p(i + 2)
+            if nxt:
+                pair_delta(nxt)
             if 0 <= i + 1 < n:
                 st_den(i + 1)
+            if nxt:
+                pair_d2(nxt)
             if 2 <= i + 3 < n:
                 st_z(i + 3, (1,))
             if 1 <= i + 2 < n:
                 st_sp(i + 2)
+            if nxt:
+                pair_e(nxt)
             if 0 <= i - 1:
                 st_sum(i - 1)
             if 3 <= i + 4 < n:
@@ -558,15 +598,16 @@ def tile_attractordepthbinhead_w4_kernel(
                         fin_copy(c - 1, range(TPC))
                 if j == 1 and c > 0:
                     fin_out(c - 1, range(TPC))
+                if i == n - 2:
+                    fin_copy(c, range(0, 2))
                 if i == n - 1:
-                    fin_copy(c, range(2))
+                    fin_out(c, range(0, 2))
+                    fin_copy(c, range(2, 3))
                 if i == n:
-                    fin_out(c, range(2))
-                    fin_copy(c, range(2, 4))
-                    fin_out(c, range(2, 4))
+                    fin_out(c, range(2, 3))
+                    fin_copy(c, range(3, 4))
+                    fin_out(c, range(3, 4))
             if i == 2:
                 plus(3)
             if 0 <= i < n and i % TPC == 0 and i // TPC + 1 < NCH:
                 turn(i // TPC + 1)
-            if 0 <= i < n and i % TPC == 1 and i // TPC + 1 < NCH:
-                pairs(i // TPC + 1)

import math
from contextlib import ExitStack

import concourse.mybir as mybir
from concourse.masks import make_identity

F32 = mybir.dt.float32
BF16 = mybir.dt.bfloat16
I32 = mybir.dt.int32
U32 = mybir.dt.uint32
U8 = mybir.dt.uint8
FP8 = mybir.dt.float8_e4m3fn
FP8X4 = mybir.dt.float8_e4m3fn_x4
FP4X4 = mybir.dt.float4_e2m1fn_x4
ALU = mybir.AluOpType
ACT = mybir.ActivationFunctionType
AX = mybir.AxisListType

P = 128
T, E, F, K = 2048, 1024, 1024, 128
CH = 512
NCH = T // CH
SPLIT = {T // P - 1}
GAIN_S = {(1, 1)}
WEIGH_S = {(0, 0), (0, 1)}
RELU_S = {0, 1}
TPC = CH // P

FLOPS = 2 * T * E * F + 2 * T * F * 2 * K


def tile_attractordepthbinhead_w4_kernel(
    tc, x_bytes, x_scale, w1_words, w1_scales, b1, g, w_head_words, w_head_scales, w_q, out
):
    nc = tc.nc
    with ExitStack() as ctx:
        const = ctx.enter_context(tc.tile_pool(name="const", bufs=1))
        work = ctx.enter_context(tc.tile_pool(name="work", bufs=2))
        psum = ctx.enter_context(tc.psum_pool(name="psum", bufs=1))
        ctx.enter_context(tc.manual_schedule(engines={mybir.EngineType.Activation}))

        w1_raw = const.tile([P, 2, 2048], U8, name="w1_raw", align_bytes=64)
        w1_perm = const.tile([P, 2, 2048], U8, name="w1_perm", align_bytes=64)
        s1_raw = const.tile([P, 2, 1024], U8, name="s1_raw", align_bytes=64)
        s1_perm = const.tile([P, 2, 1024], U8, name="s1_perm", align_bytes=64)
        wh = const.tile([P, 2, 2, 256], U8, name="wh", align_bytes=64)
        sh_raw = const.tile([P, 2, 256], U8, name="sh_raw", align_bytes=64)
        sh = const.tile([P, 2, 256], U8, name="sh", align_bytes=64)
        scale = const.tile([P, E], F32, name="scale")
        xb = const.tile([P, T // P, E], U8, name="xb")
        b1_t = const.tile([P, 8], BF16, name="b1_t")
        g_t = const.tile([P, 8], BF16, name="g_t")
        wq_t = const.tile([P, 8], BF16, name="wq_t")

        nc.vector.memset(s1_raw[:].rearrange("p g n -> p (g n)").bitcast(I32), 0)
        nc.vector.memset(sh_raw[:].rearrange("p g n -> p (g n)").bitcast(I32), 0)

        sc_col = const.tile([P, 8], F32, name="sc_col")
        nc.sync.dma_start(out=sc_col[:], in_=x_scale.rearrange("o (c p) -> p (o c)", p=P))

        def load_w1(half):
            cols = slice(1024 * half, 1024 * half + 1024)
            nc.sync.dma_start(out=w1_raw[:, :, cols], in_=w1_words[:, :, cols].rearrange("g p b -> p g b"))

        x_rows = x_bytes.rearrange("(i p) k -> p i k", p=P)
        for i in range(TPC):
            nc.sync.dma_start(out=xb[:, i, :], in_=x_rows[:, i, :])
        load_w1(0)
        for q in range(4):
            nc.sync.dma_start(
                out=s1_raw[32 * q : 32 * q + 4, :, :].rearrange("r g n -> r (g n)").bitcast(I32).rearrange("r (g n) -> r g n", g=2),
                in_=w1_scales.bitcast(I32)[:, 4 * q : 4 * q + 4, :].rearrange("g r n -> r g n"),
            )
        load_w1(1)
        nc.sync.dma_start(out=b1_t[:].rearrange("p (g t) -> p g t", g=2), in_=b1.rearrange("(g p t) -> p g t", g=2, t=4))
        nc.sync.dma_start(out=g_t[:].rearrange("p (g t) -> p g t", g=2), in_=g.rearrange("(g p t) -> p g t", g=2, t=4))
        nc.sync.dma_start(out=wq_t[:].rearrange("p (g t) -> p g t", g=2), in_=w_q.rearrange("(g p t) -> p g t", g=2, t=4))
        nc.sync.dma_start(out=xb[:, TPC : 2 * TPC, :], in_=x_rows[:, TPC : 2 * TPC, :])
        for gg in range(2):
            for h in range(2):
                nc.sync.dma_start(
                    out=wh[:, gg, h, :].rearrange("p (c b) -> p c b", c=2),
                    in_=w_head_words[gg].rearrange("p (c h b) -> p h c b", c=2, h=2)[:, h],
                )
        for q in range(4):
            nc.sync.dma_start(
                out=sh_raw[32 * q : 32 * q + 4, :, :].rearrange("r g n -> r (g n)").bitcast(I32).rearrange("r (g n) -> r g n", g=2),
                in_=w_head_scales.bitcast(I32)[:, 4 * q : 4 * q + 4, :].rearrange("g r n -> r g n"),
            )
        for c in range(2, NCH):
            nc.sync.dma_start(out=xb[:, c * TPC : (c + 1) * TPC, :], in_=x_rows[:, c * TPC : (c + 1) * TPC, :])

        kv = const.tile([P, K], F32, name="kv")
        nc.gpsimd.iota(kv[:], pattern=[[1, K]], base=0, channel_multiplier=0, allow_small_or_imprecise_dtypes=True)
        ident = const.tile([P, P], F32, name="ident")
        make_identity(nc, ident[:])
        dmat = const.tile([P, 8, 64], F32, name="dmat")
        nc.gpsimd.tensor_scalar(
            out=dmat[0:64],
            in0=ident[0:64, 0:64].unsqueeze(1).to_broadcast([64, 8, 64]),
            scalar1=-2.0, scalar2=0.0, op0=ALU.mult, op1=ALU.add,
        )
        pick = const.tile([P, 2, P], F32, name="pick")
        nc.gpsimd.memset(pick[:], 0.0)
        for h in range(2):
            nc.gpsimd.tensor_copy(out=pick[:, h, 0:64], in_=ident[:, 64 * h : 64 * h + 64])
        sel = ident[64:128, 64:128].rearrange("p (q h m) -> p m q h", h=2, m=8)
        nc.gpsimd.tensor_tensor(
            out=dmat[64:128].rearrange("p m (q i) -> p m q i", q=4),
            in0=sel[:, :, :, 0].unsqueeze(3).to_broadcast([64, 8, 4, 16]),
            in1=sel[:, :, :, 1].unsqueeze(3).to_broadcast([64, 8, 4, 16]),
            op=ALU.add,
        )
        g_f = const.tile([P, 8], F32, name="g_f")
        nc.gpsimd.tensor_copy(out=g_f[:], in_=g_t[:])
        gwq = const.tile([P, 8], F32, name="gwq")
        nc.gpsimd.tensor_tensor(out=gwq[:], in0=g_t[:], in1=wq_t[:], op=ALU.mult)
        nc.gpsimd.tensor_scalar(out=gwq[:], in0=gwq[:], scalar1=0.05, scalar2=0.0, op0=ALU.mult, op1=ALU.add)

        kk = const.tile([P, 2, K], F32, name="kk")
        kl = const.tile([P, 2, K], F32, name="kl")
        neg_lc = const.tile([P, K], F32, name="neg_lc")
        nc.vector.tensor_copy(out=kk[:, 0, :], in_=kv[:])
        nc.vector.tensor_scalar(out=kk[:, 1, :], in0=kv[:], scalar1=-1.0, scalar2=float(K - 1), op0=ALU.mult, op1=ALU.add)
        nc.vector.tensor_scalar_add(out=kk[:], in0=kk[:], scalar1=1e-6)
        nc.scalar.activation(out=kl[:], in_=kk[:], func=ACT.Ln)
        nc.vector.tensor_mul(out=kl[:], in0=kl[:], in1=kk[:])
        nc.vector.scalar_tensor_tensor(
            out=neg_lc[:], in0=kl[:, 0, :], scalar=(K - 1) * math.log(K - 1), in1=kl[:, 1, :], op0=ALU.subtract, op1=ALU.add
        )

        warm = const.tile([P, 1], F32, name="warm")
        nc.scalar.activation(out=warm[:], in_=kv[:, 0:1], func=ACT.Gelu)

        for b in range(2):
            sc_ps = psum.tile([P, 4, P], F32, name="sc_ps", tag="tr", bufs=3)
            for c in range(4):
                nc.tensor.transpose(sc_ps[:, c, :], sc_col[:, 4 * b + c : 4 * b + c + 1].to_broadcast([P, P]), ident[:])
            nc.scalar.copy(out=scale[:, 512 * b : 512 * b + 512], in_=sc_ps[:].rearrange("p c n -> p (c n)"))

        def perm_words(half):
            for gg in range(2):
                src = w1_raw[:, gg, 1024 * half : 1024 * half + 1024]
                dst = w1_perm[:, gg, 1024 * half : 1024 * half + 1024]
                nc.vector.tensor_copy(
                    out=dst.rearrange("p (t m b) -> p t m b", t=4, b=2),
                    in_=src.rearrange("p (m t b) -> p t m b", t=4, b=2),
                )

        def perm_scales():
            for gg in range(2):
                nc.vector.tensor_copy(
                    out=s1_perm[:, gg, :].rearrange("p (f t m) -> p f t m", f=2, t=4),
                    in_=s1_raw[:, gg, :].rearrange("p (f m t) -> p f t m", f=2, t=4),
                )

        def perm_head():
            nc.vector.tensor_copy(
                out=sh[:].rearrange("p g (h c n) -> p g h c n", h=2, c=2)[:, 0],
                in_=sh_raw[:].rearrange("p g (c h n) -> p g h c n", h=2, c=2)[:, 0],
            )
            nc.vector.tensor_copy(
                out=sh[:].rearrange("p g (h c n) -> p g h c n", h=2, c=2)[:, 1],
                in_=sh_raw[:].rearrange("p g (c h n) -> p g h c n", h=2, c=2)[:, 1],
            )

        xq = {}
        xc = {}
        xs = {}
        gl = {}
        hb = {}
        hz = {}
        hc = {}
        hs = {}
        yab = {}
        yt = {}
        u_sb = {}
        u_ps = {}
        qh = {}
        lg = {}
        shift = {}
        rs = {}
        weight = const.tile([P, K], F32, name="weight")

        def widen(c, j):
            if j == 0:
                xq[c] = work.tile([P, 2, CH, 4], BF16, name="xq", align_bytes=64)
            xw = work.tile([P, E], BF16, name="xw")
            nc.vector.tensor_tensor(out=xw[:], in0=xb[:, c * TPC + j, :].bitcast(FP8), in1=scale[:], op=ALU.mult)
            words = xw[:].bitcast(F32)
            xt = psum.tile([P, 2, 2, P], F32, name="xt", tag="tr", bufs=3)
            for gg in range(2):
                for u in range(2):
                    nc.tensor.transpose(xt[:, gg, u, :], words[:, 256 * gg + u : 256 * (gg + 1) : 2], ident[:])
            dst = xq[c][:].rearrange("p g n t -> p (g n t)").bitcast(F32).rearrange("p (g n u) -> p g n u", g=2, u=2)
            nc.scalar.copy(out=dst[:, :, j * P : (j + 1) * P, :], in_=xt[:].rearrange("p g u n -> p g n u"))

        def quant_x(c):
            xc[c] = work.tile([P, 2, CH], U32, name="xc", align_bytes=64, tag="m_codes", bufs=4)
            xs[c] = work.tile([P, 2, CH], U8, name="xs", align_bytes=64)
            for gg in range(2):
                nc.vector.quantize_mx(
                    out=xc[c][:, gg, :].bitcast(FP8X4), scales=xs[c][:, gg, :], in_=xq[c][:, gg].rearrange("p n t -> p (n t)")
                )

        def layer1(c, f):
            gl[c, f] = work.tile([P, 4, CH], F32, name="gl", bufs=3)
            for t in range(4):
                blk = 4 * f + t
                acc = psum.tile([P, CH], F32, name="acc", tag="s", bufs=5)
                for gg in range(2):
                    nc.tensor.matmul_mx(
                        out=acc[:],
                        lhsT=w1_perm[:, gg, 256 * blk : 256 * blk + 256].bitcast(FP4X4),
                        lhsT_scale=s1_perm[:, gg, P * blk : P * blk + P],
                        rhs=xc[c][:, gg, :].bitcast(FP8X4),
                        rhs_scale=xs[c][:, gg, :],
                        start=(gg == 0),
                        stop=(gg == 1),
                    )
                nc.scalar.activation(out=gl[c, f][:, t, :], in_=acc[:], func=ACT.Gelu, bias=b1_t[:, blk : blk + 1])

        def scale_h(c, f):
            hz[c, f] = work.tile([P, 4, CH], BF16, name="hz", align_bytes=64, tag="m_hz")
            for t in range(4):
                blk = 4 * f + t
                nc.scalar.activation(
                    out=hz[c, f][:, t, :], in_=gl[c, f][:, t, :], func=ACT.Copy, scale=g_f[:, blk : blk + 1]
                )

        def weigh(c, f):
            qh[c, f] = work.tile([P, 4, CH], F32, name="qh", bufs=4)
            for t in range(4):
                dst, src, v = qh[c, f][:, t, :], gl[c, f][:, t, :], gwq[:, 4 * f + t : 4 * f + t + 1]
                if (c, f) in WEIGH_S:
                    nc.scalar.activation(out=dst, in_=src, func=ACT.Copy, scale=v)
                else:
                    nc.vector.tensor_scalar(out=dst, in0=src, scalar1=v, scalar2=0.0, op0=ALU.mult, op1=ALU.add)

        def gain(c, f):
            hb[c, f] = work.tile([P, CH, 4], BF16, name="hb", align_bytes=64, tag="m_hb")
            if (c, f) in GAIN_S:
                nc.vector.tensor_copy(
                    out=hb[c, f][:].rearrange("p (n i) t -> p n t i", i=4),
                    in_=hz[c, f][:].rearrange("p t (n i) -> p n t i", i=4),
                )
                return
            nc.vector.tensor_tensor(
                out=hb[c, f][:].rearrange("p (n i) t -> p n t i", i=4),
                in0=gl[c, f][:].rearrange("p t (n i) -> p n t i", i=4),
                in1=g_f[:, 4 * f : 4 * f + 4].unsqueeze(1).unsqueeze(3).to_broadcast([P, CH // 4, 4, 4]),
                op=ALU.mult,
            )

        def quant_h(c, f):
            if f == 0:
                hc[c] = work.tile([P, 2, CH], U32, name="hc", align_bytes=64, tag="m_codes", bufs=4)
                hs[c] = work.tile([P, 2, CH], U8, name="hs", align_bytes=64)
            nc.vector.quantize_mx(
                out=hc[c][:, f, :].bitcast(FP8X4), scales=hs[c][:, f, :], in_=hb[c, f][:].rearrange("p n t -> p (n t)")
            )

        def layer2(c):
            yab[c] = work.tile([P, 2, CH], F32, name="yab", bufs=4)
            yt[c] = work.tile([P, 2, CH], F32, name="yt", bufs=4)
            for h in range(2):
                acc = psum.tile([P, CH], F32, name="acc", tag="s", bufs=5)
                for f in range(2):
                    nc.tensor.matmul_mx(
                        out=acc[:],
                        lhsT=wh[:, f, h, :].bitcast(FP4X4),
                        lhsT_scale=sh[:, f, P * h : P * h + P],
                        rhs=hc[c][:, f, :].bitcast(FP8X4),
                        rhs_scale=hs[c][:, f, :],
                        start=(f == 0),
                        stop=(f == 1),
                    )
                nc.scalar.activation(out=yab[c][:, h, :], in_=acc[:], func=ACT.Abs)
                if c in RELU_S:
                    nc.scalar.activation(out=yt[c][:, h, :], in_=acc[:], func=ACT.Relu)
                else:
                    nc.vector.tensor_scalar_max(out=yt[c][:, h, :], in0=acc[:], scalar1=0.0)

        def logit_u(c):
            u_ps[c] = psum.tile([P, TPC, P], F32, name="up", tag="tr", bufs=3)
            for j in range(TPC):
                for blk in range(8):
                    nc.tensor.matmul(
                        u_ps[c][:, j, :],
                        lhsT=qh[c, blk // 4][:, blk % 4, j * P : (j + 1) * P],
                        rhs=ident[:],
                        start=(blk == 0),
                        stop=(blk == 7),
                        is_transpose=True,
                    )


        def logits(c):
            u_sb[c] = work.tile([P, TPC], F32, name="u_sb", bufs=4)
            shift[c] = work.tile([P, TPC], F32, name="shift", bufs=4)
            nc.vector.tensor_reduce(out=u_sb[c][:], in_=u_ps[c][:], axis=AX.X, op=ALU.add)
            nc.vector.tensor_scalar(
                out=shift[c][:], in0=u_sb[c][:], scalar1=-float(K - 1), scalar2=0.0, op0=ALU.mult, op1=ALU.min
            )

        def weights():
            nc.scalar.activation(out=weight[:], in_=neg_lc[:], func=ACT.Exp, scale=-0.05)

        def softmax(c):
            if c % 2 == 0:
                lg[c // 2] = work.tile([P, 2 * TPC, K], F32, name="lg")
            for j in range(TPC):
                nc.scalar.activation(
                    out=lg[c // 2][:, c % 2 * TPC + j, :], in_=kv[:], func=ACT.Exp,
                    scale=u_sb[c][:, j : j + 1], bias=shift[c][:, j : j + 1],
                )

        def recips(d):
            sums = work.tile([P, 2 * TPC], F32, name="sums")
            rs[d] = work.tile([P, 2 * TPC], F32, name="rs")
            nc.vector.tensor_tensor(
                out=lg[d][:], in0=lg[d][:], in1=weight[:].unsqueeze(1).to_broadcast([P, 2 * TPC, K]), op=ALU.mult
            )
            nc.vector.tensor_reduce(out=sums[:], in_=lg[d][:], axis=AX.X, op=ALU.add)
            nc.vector.tensor_scalar_mul(out=sums[:], in0=sums[:], scalar1=1.0 / K)
            nc.vector.reciprocal(out=rs[d][:], in_=sums[:])

        def exps(c):
            nc.scalar.activation(out=yab[c][:], in_=yab[c][:], func=ACT.Exp, scale=-1.0)

        def logs(c):
            nc.scalar.activation(out=yab[c][:], in_=yab[c][:], func=ACT.Ln, bias=1.0)

        def plus(c):
            nc.vector.tensor_add(out=yt[c][:], in0=yt[c][:], in1=yab[c][:])

        ytok = {}
        d2 = {}
        ee = {}
        dl = {}

        yp = {}

        def turn_pe(c):
            for jj in range(0, TPC, 2):
                yp[c, jj] = psum.tile([P, 4, 2, 64], F32, name="yp", tag="tr", bufs=3)
                for b in range(4):
                    j, h = jj + b // 2, b % 2
                    nc.tensor.transpose(
                        yp[c, jj][:, b].rearrange("p c n -> p (c n)"), yt[c][:, h, j * P : (j + 1) * P], ident[:]
                    )

        def turn_copy(c):
            ytok[c] = work.tile([P, TPC, 2, 64], F32, name="ytok")
            for jj in range(0, TPC, 2):
                nc.scalar.copy(
                    out=ytok[c][:, jj : jj + 2].rearrange("p j h n -> p (j h) n"), in_=yp[c, jj][:, :, 1]
                )

        def turn(c):
            turn_pe(c)
            turn_copy(c)

        def pair_delta(c):
            dl[c] = work.tile([P, TPC, 8, 8], F32, name="dl")
            a = ytok[c][:].rearrange("p j h (q s m) -> p j s m (h q)", s=2, m=8)
            nc.vector.tensor_tensor(out=dl[c][:], in0=a[:, :, 0], in1=a[:, :, 1], op=ALU.subtract)

        def pair_d2(c):
            d2[c] = work.tile([P, TPC, 8, 8], F32, name="d2")
            nc.vector.scalar_tensor_tensor(out=d2[c][:], in0=dl[c][:], scalar=2.0, in1=dl[c][:], op0=ALU.mult, op1=ALU.mult)

        def pair_e(c):
            ee[c] = work.tile([P, TPC, 8, 8], F32, name="ee")
            nc.vector.tensor_scalar(out=ee[c][:], in0=d2[c][:], scalar1=-0.25, scalar2=1.0, op0=ALU.mult, op1=ALU.add)

        ss = {}
        zz = {}
        pp = {}
        qq = {}
        sp = {}
        cp = {}
        cs = {}

        def st_s(i):
            c, j = divmod(i, TPC)
            for h in range(2):
                ss[i, h] = psum.tile([P, 512], F32, name="s_ps", tag="s", bufs=5)
                nc.tensor.matmul(
                    ss[i, h][:], lhsT=yt[c][:, h, j * P : (j + 1) * P], rhs=dmat[:].rearrange("p m n -> p (m n)"),
                    start=True, stop=True,
                )

        def st_z(i, halves=(0, 1)):
            if halves[0] == 0:
                zz[i] = work.tile([P, 8, 2, 64], F32, name="zz", align_bytes=64, tag="m_hb")
            for h in halves:
                nc.scalar.activation(
                    out=zz[i][:, :, h, :], in_=ss[i, h][:].rearrange("p (m n) -> p m n", m=8), func=ACT.Square, scale=math.sqrt(0.5)
                )

        def parts(i):
            return [slice(0, 4), slice(4, 8)] if i in SPLIT else [slice(0, 8)]

        def rows(ap):
            return ap.rearrange("p m h (q i) -> p (m h q) i", q=4)

        def spread(ap):
            w = ap.rearrange("p m n -> p (m n)")
            return w.unsqueeze(2).to_broadcast([P, w.shape[1], 16])

        def st_den(i):
            c, j = divmod(i, TPC)
            for m in parts(i):
                q3 = rows(qq[i][:, m])
                nc.vector.tensor_tensor(out=q3, in0=q3, in1=spread(d2[c][:, j, m]), op=ALU.add)
                nc.scalar.activation(out=qq[i][:, m], in_=qq[i][:, m], func=ACT.Abs_reciprocal_sqrt)

        def st_p(i):
            c, j = divmod(i, TPC)
            pp[i] = work.tile([P, 8, 2, 64], F32, name="pp", align_bytes=64, tag="m_hz")
            qq[i] = work.tile([P, 8, 2, 64], F32, name="qq", bufs=3)
            sp[i] = work.tile([P, 8, 2, 64], F32, name="sp", align_bytes=64, tag="m_codes", bufs=4)
            for m in parts(i):
                nc.vector.tensor_tensor(
                    out=rows(pp[i][:, m]), in0=rows(zz[i][:, m]), in1=spread(ee[c][:, j, m]), op=ALU.add
                )
                nc.scalar.activation(out=qq[i][:, m], in_=pp[i][:, m], func=ACT.Square)

        def st_sp(i):
            for h in range(2):
                nc.vector.scalar_tensor_tensor(
                    out=sp[i][:, :, h, :], in0=ss[i, h][:].rearrange("p (m n) -> p m n", m=8), scalar=0.125,
                    in1=pp[i][:, :, h, :], op0=ALU.mult, op1=ALU.mult,
                )

        def st_r(i):
            for m in parts(i):
                nc.scalar.activation(out=qq[i][:, m], in_=qq[i][:, m], func=ACT.Square)

        def st_f(i):
            for m in parts(i):
                nc.vector.tensor_mul(out=sp[i][:, m], in0=sp[i][:, m], in1=qq[i][:, m])

        def st_sum(i):
            c, j = divmod(i, TPC)
            if j == 0:
                cp[c] = psum.tile([P, TPC, P], F32, name="cp", tag="tr", bufs=3)
            for m in range(8):
                nc.tensor.matmul(
                    cp[c][:, j, :], lhsT=sp[i][:, m].rearrange("p h n -> p (h n)"), rhs=ident[:], start=(m == 0), stop=(m == 7),
                    is_transpose=True,
                )

        out_rows = out.rearrange("(c j p) k -> c p j k", p=P, j=TPC)

        ot = {}
        c2 = {}

        def fin_copy(c, js):
            if js[0] == 0:
                cs[c] = work.tile([P, TPC, P], F32, name="cs")
                ot[c] = work.tile([P, TPC, K], F32, name="ot")
            sl = slice(js[0], js[-1] + 1)
            nc.scalar.copy(out=cs[c][:, sl, :], in_=cp[c][:, sl, :])
            for j in js:
                if j % 2 == 0:
                    c2[c, j // 2] = psum.tile([P, 2, 2, P], F32, name="c2", tag="tr", bufs=3)
                for h in range(2):
                    dst = c2[c, j // 2][:, j % 2, h, :]
                    nc.tensor.matmul(dst, lhsT=cs[c][:, j, :], rhs=pick[:, h, :], start=True, stop=False, is_transpose=True)
                    nc.tensor.matmul(
                        dst, lhsT=yt[c][:, h, j * P : (j + 1) * P], rhs=ident[:], start=False, stop=True, is_transpose=True
                    )

        def fin_out(c, js):
            sl = slice(js[0], js[-1] + 1)
            for j in js:
                nc.vector.scalar_tensor_tensor(
                    out=ot[c][:, j, :].rearrange("p (h n) -> p h n", h=2), in0=lg[c // 2][:, c % 2 * TPC + j, :].rearrange("p (h n) -> p h n", h=2),
                    scalar=rs[c // 2][:, c % 2 * TPC + j : c % 2 * TPC + j + 1],
                    in1=c2[c, j // 2][:, j % 2, :, 0:64], op0=ALU.mult, op1=ALU.mult,
                )
            nc.sync.dma_start(out=out_rows[c][:, sl, :], in_=ot[c][:, sl, :])

        for j in range(TPC):
            widen(0, j)
        perm_scales()
        widen(1, 0)
        widen(1, 1)
        perm_words(0)
        widen(1, 2)
        for c in range(NCH):
            quant_x(c)
            if c > 1:
                logit_u(c - 2)
            if c > 2:
                logits(c - 3)
            if (c - 1, 1) in GAIN_S:
                scale_h(c - 1, 1)
            if c > 0 and (c - 1, 1) not in GAIN_S:
                gain(c - 1, 1)
            layer1(c, 0)
            weigh(c, 0)
            if c == 0:
                perm_words(1)
            if c + 1 < NCH:
                widen(c + 1, 3)
            if (c - 1, 1) in GAIN_S:
                gain(c - 1, 1)
            if c > 0:
                quant_h(c - 1, 1)
            gain(c, 0)
            if c == 0:
                perm_head()
            if c == 1:
                layer2(0)
            if c + 2 < NCH:
                widen(c + 2, 0)
                widen(c + 2, 1)
            layer1(c, 1)
            if c == 2:
                layer2(1)
            weigh(c, 1)
            quant_h(c, 0)
            if c + 2 < NCH:
                widen(c + 2, 2)
        weights()
        logits(NCH - 3)
        logit_u(NCH - 2)
        exps(0)
        exps(1)
        logit_u(NCH - 1)
        layer2(NCH - 2)
        logits(NCH - 2)
        softmax(0)
        logits(NCH - 1)
        gain(NCH - 1, 1)
        exps(NCH - 2)
        quant_h(NCH - 1, 1)
        softmax(1)
        softmax(2)
        layer2(NCH - 1)
        softmax(3)
        exps(NCH - 1)
        logs(0)
        plus(0)
        logs(1)
        turn_pe(0)
        st_s(0)
        logs(2)
        turn_copy(0)
        pair_delta(0)
        plus(1)
        pair_d2(0)
        logs(3)
        st_s(1)
        st_z(0)
        recips(0)
        pair_e(0)
        st_z(1)
        st_p(0)
        plus(2)
        st_sp(0)
        recips(1)
        st_s(2)
        n = T // P
        for i in range(-1, n + 1):
            nxt = i // TPC + 1 if 0 <= i < n and i % TPC == 1 and i // TPC + 1 < NCH else 0
            if 2 <= i + 3 < n:
                st_z(i + 3, (0,))
            if 1 <= i + 2 < n:
                st_p(i + 2)
            if nxt:
                pair_delta(nxt)
            if 0 <= i + 1 < n:
                st_den(i + 1)
            if nxt:
                pair_d2(nxt)
            if 2 <= i + 3 < n:
                st_z(i + 3, (1,))
            if 1 <= i + 2 < n:
                st_sp(i + 2)
            if nxt:
                pair_e(nxt)
            if 0 <= i - 1:
                st_sum(i - 1)
            if 3 <= i + 4 < n:
                st_s(i + 4)
            if 0 <= i + 1 < n:
                st_r(i + 1)
            if 0 <= i < n:
                st_f(i)
            if i >= 1:
                c, j = divmod(i - 1, TPC)
                if j == 0:
                    if c > 0:
                        fin_copy(c - 1, range(TPC))
                if j == 1 and c > 0:
                    fin_out(c - 1, range(TPC))
                if i == n - 2:
                    fin_copy(c, range(0, 2))
                if i == n - 1:
                    fin_out(c, range(0, 2))
                    fin_copy(c, range(2, 3))
                if i == n:
                    fin_out(c, range(2, 3))
                    fin_copy(c, range(3, 4))
                    fin_out(c, range(3, 4))
            if i == 2:
                plus(3)
            if 0 <= i < n and i % TPC == 0 and i // TPC + 1 < NCH:
                turn(i // TPC + 1)
